import numpy as np
import ml_dtypes


def mxq(x, axis, fmt="e4m3"):
    dtype, down = {"e4m3": (ml_dtypes.float8_e4m3fn, 7), "e5m2": (ml_dtypes.float8_e5m2, 14)}[fmt]
    v = np.moveaxis(np.asarray(x, np.float32).astype(ml_dtypes.bfloat16).astype(np.float64), axis, -1)
    blocks = v.reshape(v.shape[:-1] + (-1, 32))
    amax = np.abs(blocks).max(-1, keepdims=True)
    byte = np.maximum(np.where(amax > 0, np.frexp(amax)[1] - 1 + 127, 0) - down, 1)
    scale = np.exp2(byte - 127.0)
    codes = (blocks / scale).astype(np.float32).astype(dtype).astype(np.float64)
    return np.moveaxis((codes * scale).reshape(v.shape), -1, axis)


WIDE = False


def mx_kscale(k):
    if not WIDE:
        return np.ones(k)
    levels = np.array([24, -24, 12, -12, 0])
    if k % 512:
        return np.exp2(np.random.permutation(np.resize(levels, k // 32))).repeat(32)
    a = np.empty((k // 512, 16))
    for p in range(k // 512):
        a[p, :8] = np.random.permutation(np.resize(levels, 8))
        for g in range(8):
            far = levels[np.abs(levels - a[p, g]) >= 10]
            a[p, g + 8] = far[np.random.randint(len(far))]
    return np.exp2(a.ravel()).repeat(32)


def f64(x):
    return np.asarray(x).astype(np.float64)


E2M1 = np.array([0.0, 0.5, 1.0, 1.5, 2.0, 3.0, 4.0, 6.0, -0.0, -0.5, -1.0, -1.5, -2.0, -3.0, -4.0, -6.0])


def pack_weight(w, fmt):
    k, n = w.shape
    w = f64(np.asarray(w, np.float32).astype(ml_dtypes.bfloat16)).reshape(k // 32, 32, n)
    amax = np.abs(w).max(1)
    if fmt == "e4m3":
        byte = np.frexp(amax)[1] - 1 + 127 - 7
    else:
        mant, ex = np.frexp(amax / 6.0)
        byte = np.where(mant > 0.5, ex, ex - 1) + 127
    byte = np.clip(np.where(amax > 0, byte, 1), 1, 254)
    scaled = (w * np.exp2(127.0 - byte)[:, None, :]).reshape(k, n).astype(np.float32)
    by_word = np.ascontiguousarray(scaled.reshape(k // 512, 128, 4, n).transpose(0, 1, 3, 2))
    if fmt == "e4m3":
        words = by_word.astype(ml_dtypes.float8_e4m3fn).view(np.uint8)
    else:
        c = by_word.astype(ml_dtypes.float4_e2m1fn).view(np.uint8) & 0xF
        words = (c[..., 0::2] | (c[..., 1::2] << 4)).reshape(k // 512, 128, 2 * n)
    return np.ascontiguousarray(words), np.ascontiguousarray(byte.astype(np.uint8).reshape(k // 512, 16, n))


def unpack_weight(words, scales, fmt):
    g, _, n = scales.shape
    words = np.ascontiguousarray(words).reshape(g, 128, n, -1)
    if fmt == "e4m3":
        vals = words.view(ml_dtypes.float8_e4m3fn).astype(np.float64)
    else:
        nib = np.empty((g, 128, n, 4), np.uint8)
        nib[..., 0::2] = words & 0xF
        nib[..., 1::2] = words >> 4
        vals = E2M1[nib]
    vals = vals * np.repeat(np.exp2(scales.astype(np.float64) - 127.0), 8, axis=1)[..., None]
    return vals.transpose(0, 1, 3, 2).reshape(g * 512, n)


def planes(y):
    n, m = y.shape
    v = y.astype(np.float32).astype(ml_dtypes.bfloat16).astype(np.float64).reshape(n // 32, 32, m)
    top = np.abs(v).max(1)
    byte = np.clip(np.where(top > 0, np.frexp(top)[1] - 1 + 127 - 7, 1), 1, 254)
    codes = (v * np.exp2(127.0 - byte)[:, None, :]).reshape(n, m).astype(np.float32).astype(ml_dtypes.float8_e4m3fn).view(np.uint8)
    words = codes.reshape(n // 512, 128, 4, m).transpose(0, 1, 3, 2)
    return np.ascontiguousarray(words), np.ascontiguousarray(byte.astype(np.uint8).reshape(n // 512, 16, m))


K, D, M, J = 512, 512, 512, 512


def setup_inputs():
    n = np.random.standard_normal
    u = mx_kscale(D)[:, None]
    s3 = mx_kscale(K)[:, None]
    s = mx_kscale(K)[:, None]
    p_w8 = pack_weight(n((K, D)) / np.sqrt(K) / s / u.T, "e4m3")
    p_wk = pack_weight(n((K, D)) / np.sqrt(K) / s3 * u.T, "e2m1")
    return {
        "x": (n((K, M)) * s).astype(np.float32),
        "w8_words": p_w8[0],
        "w8_scales": p_w8[1],
        "c": (n((K, J)) * s3).astype(np.float32),
        "wk_words": p_wk[0],
        "wk_scales": p_wk[1],
    }


def reference(x, w8_words, w8_scales, c, wk_words, wk_scales):
    x_ = mxq(f64(x), 0, "e4m3")
    w8_ = unpack_weight(w8_words, w8_scales, "e4m3")
    qr = w8_.T @ x_
    qr_ = mxq(qr, 0, "e4m3")
    c_ = mxq(f64(c), 0, "e4m3")
    wk_ = unpack_weight(wk_words, wk_scales, "e2m1")
    kc = wk_.T @ c_
    kc_ = mxq(kc, 0, "e4m3")
    sc = qr_.T @ kc_
    return (np.maximum(sc, 0.0) * 0.03125, kc) + planes(kc)

@@ -1,0 +1,239 @@
+from contextlib import ExitStack
+
+import concourse.mybir as mybir
+
+K, D, M, J = 512, 512, 512, 512
+FLOPS = 2 * (K * D * M + K * D * J + D * M * J)
+
+F32 = mybir.dt.float32
+BF16 = mybir.dt.bfloat16
+I32 = mybir.dt.int32
+U32 = mybir.dt.uint32
+U8 = mybir.dt.uint8
+FP8X4 = mybir.dt.float8_e4m3fn_x4
+FP4X4 = mybir.dt.float4_e2m1fn_x4
+ACT = mybir.ActivationFunctionType
+ALU = mybir.AluOpType
+
+P = 128
+PACK = 4
+QUARTER = 128
+HALF = 256
+SCORE_SCALE = 0.03125
+
+
+def tile_mix_kvw_relu_kernel(
+    tc, x, w8_words, w8_scales, c, wk_words, wk_scales, out_0, out_1, out_2, out_3
+):
+    nc = tc.nc
+    with ExitStack() as ctx:
+        sb = ctx.enter_context(tc.tile_pool(name="sb", bufs=1))
+        ps = ctx.enter_context(tc.psum_pool(name="ps", bufs=1))
+        ctx.enter_context(tc.manual_schedule())
+
+        def tiles(name, count, shape, dtype):
+            return [sb.tile(shape, dtype, name="%s%d" % (name, i), align_bytes=64) for i in range(count)]
+
+        wk_raw = sb.tile([P, 2 * D], U8, align_bytes=64)
+        w8_raw = sb.tile([P, D], I32, align_bytes=64)
+        scales_raw = sb.tile([P, 2 * D], U8, align_bytes=64)
+        wk_codes = sb.tile([P, 2 * D], U8, align_bytes=64)
+        wk_plane = sb.tile([P, D], U8, align_bytes=64)
+        w8_codes = sb.tile([P, D], I32, align_bytes=64)
+        w8_plane = sb.tile([P, D], U8, align_bytes=64)
+        c_raw = tiles("c_raw", 2, [P, PACK, HALF], F32)
+        x_raw = tiles("x_raw", 2, [P, PACK, HALF], F32)
+        c_bf = tiles("c_bf", 4, [P, QUARTER * PACK], BF16)
+        x_bf = tiles("x_bf", 4, [P, QUARTER * PACK], BF16)
+        c_codes = tiles("c_codes", 4, [P, QUARTER], U32)
+        c_plane = tiles("c_plane", 4, [P, QUARTER], U8)
+        x_codes = tiles("x_codes", 4, [P, QUARTER], U32)
+        x_plane = tiles("x_plane", 4, [P, QUARTER], U8)
+        kc_f32 = tiles("kc_f32", 2, [P, PACK, HALF], F32)
+        kc_bf = tiles("kc_bf", 2, [P, HALF * PACK], BF16)
+        kc_codes = sb.tile([P, J], U32, align_bytes=64)
+        kc_plane = sb.tile([P, J], U8, align_bytes=64)
+        qr_bf = tiles("qr_bf", 4, [P, QUARTER * PACK], BF16)
+        qr_codes = tiles("qr_codes", 4, [P, QUARTER], U32)
+        qr_plane = tiles("qr_plane", 4, [P, QUARTER], U8)
+        scores = tiles("scores", 4, [P, J], F32)
+        kc_ps = {}
+        qr_ps = {}
+        sc_ps = {}
+
+        def load_scale_rows(dram, col0):
+            rows = dram[0].bitcast(I32)
+            for q in range(4):
+                nc.sync.dma_start(
+                    out=scales_raw[32 * q : 32 * q + 4, col0 : col0 + D].bitcast(I32),
+                    in_=rows[4 * q : 4 * q + 4, :],
+                )
+
+        def load_half(raw, dram, h):
+            view = dram.rearrange("(p t) n -> p t n", t=PACK)
+            nc.sync.dma_start(out=raw[h][:], in_=view[:, :, h * HALF : (h + 1) * HALF])
+
+        def deal_plane(plane, col0):
+            nc.vector.tensor_copy(
+                out=plane[:].rearrange("p (t g i) -> p g t i", t=PACK, i=16),
+                in_=scales_raw[:, col0 : col0 + D].rearrange("p (g i t) -> p g t i", t=PACK, i=16),
+            )
+
+        def interleave(engine, dst, src):
+            out = dst.rearrange("p (g i t) -> p g t i", t=PACK, i=2)
+            in_ = src.rearrange("p t (g i) -> p g t i", i=2)
+            if engine == "vector":
+                nc.vector.tensor_copy(out=out, in_=in_)
+            else:
+                nc.scalar.activation(out=out, in_=in_, func=ACT.Copy)
+
+        def round_quarter(engine, bf, raw, q):
+            cols = slice((q % 2) * QUARTER, (q % 2 + 1) * QUARTER)
+            interleave(engine, bf[q][:], raw[q // 2][:, :, cols])
+
+        def quantize(codes, plane, bf):
+            nc.vector.quantize_mx(out=codes.bitcast(FP8X4), scales=plane, in_=bf)
+
+        def project_keys(q):
+            kc_ps[q] = ps.tile([P, PACK, QUARTER], F32, name="bank_a%d" % q)
+            for t in range(PACK):
+                nc.tensor.matmul_mx(
+                    out=kc_ps[q][:, t, :],
+                    lhsT=wk_codes[:, 2 * P * t : 2 * P * (t + 1)].bitcast(FP4X4),
+                    lhsT_scale=wk_plane[:, P * t : P * (t + 1)],
+                    rhs=c_codes[q][:].bitcast(FP8X4),
+                    rhs_scale=c_plane[q][:],
+                    start=True,
+                    stop=True,
+                )
+
+        def project_queries(q):
+            qr_ps[q] = ps.tile([P, PACK, QUARTER], F32, name="bank_b%d" % q)
+            for t in range(PACK):
+                nc.tensor.matmul_mx(
+                    out=qr_ps[q][:, t, :],
+                    lhsT=w8_codes[:, P * t : P * (t + 1)].bitcast(FP8X4),
+                    lhsT_scale=w8_plane[:, P * t : P * (t + 1)],
+                    rhs=x_codes[q][:].bitcast(FP8X4),
+                    rhs_scale=x_plane[q][:],
+                    start=True,
+                    stop=True,
+                )
+
+        def score(q):
+            sc_ps[q] = ps.tile([P, J], F32, name="bank_a%d" % q)
+            nc.tensor.matmul_mx(
+                out=sc_ps[q][:],
+                lhsT=qr_codes[q][:].bitcast(FP8X4),
+                lhsT_scale=qr_plane[q][:],
+                rhs=kc_codes[:].bitcast(FP8X4),
+                rhs_scale=kc_plane[:],
+                start=True,
+                stop=True,
+            )
+
+        def drain_keys(q):
+            cols = slice((q % 2) * QUARTER, (q % 2 + 1) * QUARTER)
+            nc.scalar.copy(out=kc_f32[q // 2][:, :, cols], in_=kc_ps[q][:])
+
+        def drain_queries(q):
+            nc.scalar.copy(
+                out=qr_bf[q][:].rearrange("p (n t) -> p n t", t=PACK),
+                in_=qr_ps[q][:].rearrange("p t n -> p n t"),
+            )
+
+        def drain_scores(engine, q):
+            if engine == "vector":
+                nc.vector.tensor_scalar(
+                    out=scores[q][:], in0=sc_ps[q][:], scalar1=0.0, scalar2=SCORE_SCALE, op0=ALU.max, op1=ALU.mult
+                )
+            else:
+                nc.scalar.activation(out=scores[q][:], in_=sc_ps[q][:], func=ACT.Relu, scale=SCORE_SCALE)
+            nc.sync.dma_start(out=out_0[q * QUARTER : (q + 1) * QUARTER, :], in_=scores[q][:])
+
+        def store_keys(h):
+            view = out_1.rearrange("(p t) n -> p t n", t=PACK)
+            nc.sync.dma_start(out=view[:, :, h * HALF : (h + 1) * HALF], in_=kc_f32[h][:])
+
+        def quantize_keys(h):
+            cols = slice(h * HALF, (h + 1) * HALF)
+            quantize(kc_codes[:, cols], kc_plane[:, cols], kc_bf[h][:])
+
+        nc.vector.memset(scales_raw[:].bitcast(I32), 0)
+        nc.sync.dma_start(out=wk_raw[:].bitcast(I32), in_=wk_words[0].bitcast(I32))
+        load_half(c_raw, c, 0)
+        load_scale_rows(wk_scales, 0)
+        load_half(c_raw, c, 1)
+        nc.sync.dma_start(out=w8_raw[:], in_=w8_words[0].rearrange("p n t -> p (n t)").bitcast(I32))
+        load_scale_rows(w8_scales, D)
+        load_half(x_raw, x, 0)
+        load_half(x_raw, x, 1)
+
+        nc.vector.tensor_copy(
+            out=wk_codes[:].rearrange("p (t g i b) -> p g t i b", t=PACK, i=8, b=2),
+            in_=wk_raw[:].rearrange("p (g i t b) -> p g t i b", t=PACK, i=8, b=2),
+        )
+        round_quarter("vector", c_bf, c_raw, 0)
+        round_quarter("scalar", c_bf, c_raw, 1)
+        deal_plane(wk_plane, 0)
+        quantize(c_codes[0][:], c_plane[0][:], c_bf[0][:])
+        project_keys(0)
+        quantize(c_codes[1][:], c_plane[1][:], c_bf[1][:])
+        project_keys(1)
+        round_quarter("vector", c_bf, c_raw, 2)
+        round_quarter("vector", c_bf, c_raw, 3)
+        drain_keys(0)
+        drain_keys(1)
+        store_keys(0)
+        quantize(c_codes[2][:], c_plane[2][:], c_bf[2][:])
+        project_keys(2)
+        quantize(c_codes[3][:], c_plane[3][:], c_bf[3][:])
+        project_keys(3)
+        drain_keys(2)
+        drain_keys(3)
+        store_keys(1)
+        nc.vector.tensor_copy(
+            out=w8_codes[:].rearrange("p (t g i) -> p g t i", t=PACK, i=4),
+            in_=w8_raw[:].rearrange("p (g i t) -> p g t i", t=PACK, i=4),
+        )
+        deal_plane(w8_plane, D)
+        interleave("vector", kc_bf[0][:], kc_f32[0][:])
+        round_quarter("vector", x_bf, x_raw, 0)
+        quantize_keys(0)
+        round_quarter("vector", x_bf, x_raw, 1)
+        quantize(x_codes[0][:], x_plane[0][:], x_bf[0][:])
+        project_queries(0)
+        quantize(x_codes[1][:], x_plane[1][:], x_bf[1][:])
+        project_queries(1)
+        drain_queries(0)
+        drain_queries(1)
+        interleave("vector", kc_bf[1][:], kc_f32[1][:])
+        round_quarter("vector", x_bf, x_raw, 2)
+        quantize_keys(1)
+        nc.sync.dma_start(
+            out=out_2[0].rearrange("p n t -> p (n t)").bitcast(I32), in_=kc_codes[:].bitcast(I32)
+        )
+        plane_rows = out_3[0].bitcast(I32)
+        for q in range(4):
+            nc.sync.dma_start(
+                out=plane_rows[4 * q : 4 * q + 4, :], in_=kc_plane[32 * q : 32 * q + 4, :].bitcast(I32)
+            )
+        round_quarter("vector", x_bf, x_raw, 3)
+        quantize(x_codes[2][:], x_plane[2][:], x_bf[2][:])
+        project_queries(2)
+        quantize(qr_codes[0][:], qr_plane[0][:], qr_bf[0][:])
+        score(0)
+        quantize(x_codes[3][:], x_plane[3][:], x_bf[3][:])
+        project_queries(3)
+        quantize(qr_codes[1][:], qr_plane[1][:], qr_bf[1][:])
+        score(1)
+        drain_queries(2)
+        drain_queries(3)
+        drain_scores("vector", 0)
+        quantize(qr_codes[2][:], qr_plane[2][:], qr_bf[2][:])
+        score(2)
+        drain_scores("vector", 1)
+        quantize(qr_codes[3][:], qr_plane[3][:], qr_bf[3][:])
+        score(3)
+        drain_scores("scalar", 2)
+        drain_scores("vector", 3)

@@ -50,7 +50,7 @@ def tile_mix_kvw_relu_kernel(
         x_codes = tiles("x_codes", 4, [P, QUARTER], U32)
         x_plane = tiles("x_plane", 4, [P, QUARTER], U8)
         kc_f32 = tiles("kc_f32", 2, [P, PACK, HALF], F32)
-        kc_bf = tiles("kc_bf", 2, [P, HALF * PACK], BF16)
+        kc_bf = tiles("kc_bf", 4, [P, QUARTER * PACK], BF16)
         kc_codes = sb.tile([P, J], U32, align_bytes=64)
         kc_plane = sb.tile([P, J], U8, align_bytes=64)
         qr_bf = tiles("qr_bf", 4, [P, QUARTER * PACK], BF16)
@@ -136,11 +136,13 @@ def tile_mix_kvw_relu_kernel(
             cols = slice((q % 2) * QUARTER, (q % 2 + 1) * QUARTER)
             nc.scalar.copy(out=kc_f32[q // 2][:, :, cols], in_=kc_ps[q][:])
 
-        def drain_queries(q):
-            nc.scalar.copy(
-                out=qr_bf[q][:].rearrange("p (n t) -> p n t", t=PACK),
-                in_=qr_ps[q][:].rearrange("p t n -> p n t"),
-            )
+        def drain_queries(engine, q):
+            out = qr_bf[q][:].rearrange("p (n t) -> p n t", t=PACK)
+            in_ = qr_ps[q][:].rearrange("p t n -> p n t")
+            if engine == "vector":
+                nc.vector.tensor_copy(out=out, in_=in_)
+            else:
+                nc.scalar.copy(out=out, in_=in_)
 
         def drain_scores(engine, q):
             if engine == "vector":
@@ -149,15 +151,17 @@ def tile_mix_kvw_relu_kernel(
                 )
             else:
                 nc.scalar.activation(out=scores[q][:], in_=sc_ps[q][:], func=ACT.Relu, scale=SCORE_SCALE)
+
+        def store_scores(q):
             nc.sync.dma_start(out=out_0[q * QUARTER : (q + 1) * QUARTER, :], in_=scores[q][:])
 
         def store_keys(h):
             view = out_1.rearrange("(p t) n -> p t n", t=PACK)
             nc.sync.dma_start(out=view[:, :, h * HALF : (h + 1) * HALF], in_=kc_f32[h][:])
 
-        def quantize_keys(h):
-            cols = slice(h * HALF, (h + 1) * HALF)
-            quantize(kc_codes[:, cols], kc_plane[:, cols], kc_bf[h][:])
+        def quantize_keys(q):
+            cols = slice(q * QUARTER, (q + 1) * QUARTER)
+            quantize(kc_codes[:, cols], kc_plane[:, cols], kc_bf[q][:])
 
         nc.vector.memset(scales_raw[:].bitcast(I32), 0)
         nc.sync.dma_start(out=wk_raw[:].bitcast(I32), in_=wk_words[0].bitcast(I32))
@@ -168,7 +172,6 @@ def tile_mix_kvw_relu_kernel(
         load_scale_rows(w8_scales, D)
         load_half(x_raw, x, 0)
         load_half(x_raw, x, 1)
-
         nc.vector.tensor_copy(
             out=wk_codes[:].rearrange("p (t g i b) -> p g t i b", t=PACK, i=8, b=2),
             in_=wk_raw[:].rearrange("p (g i t b) -> p g t i b", t=PACK, i=8, b=2),
@@ -181,59 +184,62 @@ def tile_mix_kvw_relu_kernel(
         quantize(c_codes[1][:], c_plane[1][:], c_bf[1][:])
         project_keys(1)
         round_quarter("vector", c_bf, c_raw, 2)
-        round_quarter("vector", c_bf, c_raw, 3)
-        drain_keys(0)
-        drain_keys(1)
-        store_keys(0)
+        round_quarter("scalar", c_bf, c_raw, 3)
         quantize(c_codes[2][:], c_plane[2][:], c_bf[2][:])
         project_keys(2)
-        quantize(c_codes[3][:], c_plane[3][:], c_bf[3][:])
-        project_keys(3)
-        drain_keys(2)
-        drain_keys(3)
-        store_keys(1)
+        drain_keys(0)
         nc.vector.tensor_copy(
             out=w8_codes[:].rearrange("p (t g i) -> p g t i", t=PACK, i=4),
             in_=w8_raw[:].rearrange("p (g i t) -> p g t i", t=PACK, i=4),
         )
+        quantize(c_codes[3][:], c_plane[3][:], c_bf[3][:])
+        project_keys(3)
+        drain_keys(1)
         deal_plane(w8_plane, D)
-        interleave("vector", kc_bf[0][:], kc_f32[0][:])
+        round_quarter("vector", kc_bf, kc_f32, 0)
+        drain_keys(2)
+        store_keys(0)
+        drain_keys(3)
+        store_keys(1)
         round_quarter("vector", x_bf, x_raw, 0)
-        quantize_keys(0)
         round_quarter("vector", x_bf, x_raw, 1)
         quantize(x_codes[0][:], x_plane[0][:], x_bf[0][:])
         project_queries(0)
         quantize(x_codes[1][:], x_plane[1][:], x_bf[1][:])
         project_queries(1)
-        drain_queries(0)
-        drain_queries(1)
-        interleave("vector", kc_bf[1][:], kc_f32[1][:])
+        round_quarter("scalar", kc_bf, kc_f32, 2)
+        round_quarter("scalar", kc_bf, kc_f32, 3)
+        round_quarter("vector", kc_bf, kc_f32, 1)
         round_quarter("vector", x_bf, x_raw, 2)
-        quantize_keys(1)
-        nc.sync.dma_start(
-            out=out_2[0].rearrange("p n t -> p (n t)").bitcast(I32), in_=kc_codes[:].bitcast(I32)
-        )
-        plane_rows = out_3[0].bitcast(I32)
-        for q in range(4):
-            nc.sync.dma_start(
-                out=plane_rows[4 * q : 4 * q + 4, :], in_=kc_plane[32 * q : 32 * q + 4, :].bitcast(I32)
-            )
+        quantize_keys(0)
         round_quarter("vector", x_bf, x_raw, 3)
         quantize(x_codes[2][:], x_plane[2][:], x_bf[2][:])
         project_queries(2)
-        quantize(qr_codes[0][:], qr_plane[0][:], qr_bf[0][:])
-        score(0)
+        quantize_keys(1)
         quantize(x_codes[3][:], x_plane[3][:], x_bf[3][:])
         project_queries(3)
+        quantize_keys(2)
+        quantize_keys(3)
+        nc.sync.dma_start(out=out_2[0].rearrange("p n t -> p (n t)").bitcast(I32), in_=kc_codes[:].bitcast(I32))
+        for q in range(4):
+            nc.sync.dma_start(out=out_3[0].bitcast(I32)[4 * q : 4 * q + 4, :], in_=kc_plane[32 * q : 32 * q + 4, :].bitcast(I32))
+        drain_queries("scalar", 0)
+        drain_queries("scalar", 1)
+        quantize(qr_codes[0][:], qr_plane[0][:], qr_bf[0][:])
+        score(0)
         quantize(qr_codes[1][:], qr_plane[1][:], qr_bf[1][:])
         score(1)
-        drain_queries(2)
-        drain_queries(3)
-        drain_scores("vector", 0)
+        drain_queries("scalar", 2)
+        drain_queries("vector", 3)
+        drain_scores("scalar", 0)
+        store_scores(0)
         quantize(qr_codes[2][:], qr_plane[2][:], qr_bf[2][:])
         score(2)
-        drain_scores("vector", 1)
         quantize(qr_codes[3][:], qr_plane[3][:], qr_bf[3][:])
         score(3)
+        drain_scores("vector", 1)
+        store_scores(1)
         drain_scores("scalar", 2)
+        store_scores(2)
         drain_scores("vector", 3)
+        store_scores(3)

@@ -9,6 +9,7 @@ F32 = mybir.dt.float32
 BF16 = mybir.dt.bfloat16
 I32 = mybir.dt.int32
 U32 = mybir.dt.uint32
+U16 = mybir.dt.uint16
 U8 = mybir.dt.uint8
 FP8X4 = mybir.dt.float8_e4m3fn_x4
 FP4X4 = mybir.dt.float4_e2m1fn_x4
@@ -30,216 +31,223 @@ def tile_mix_kvw_relu_kernel(
         sb = ctx.enter_context(tc.tile_pool(name="sb", bufs=1))
         ps = ctx.enter_context(tc.psum_pool(name="ps", bufs=1))
         ctx.enter_context(tc.manual_schedule())
+        queue = {"sync": nc.sync, "scalar": nc.scalar}
 
-        def tiles(name, count, shape, dtype):
-            return [sb.tile(shape, dtype, name="%s%d" % (name, i), align_bytes=64) for i in range(count)]
+        def tile(name, shape, dtype):
+            return sb.tile(shape, dtype, name=name, align_bytes=64)
 
-        wk_raw = sb.tile([P, 2 * D], U8, align_bytes=64)
-        w8_raw = sb.tile([P, D], I32, align_bytes=64)
-        scales_raw = sb.tile([P, 2 * D], U8, align_bytes=64)
-        wk_codes = sb.tile([P, 2 * D], U8, align_bytes=64)
-        wk_plane = sb.tile([P, D], U8, align_bytes=64)
-        w8_codes = sb.tile([P, D], I32, align_bytes=64)
-        w8_plane = sb.tile([P, D], U8, align_bytes=64)
-        c_raw = tiles("c_raw", 2, [P, PACK, HALF], F32)
-        x_raw = tiles("x_raw", 2, [P, PACK, HALF], F32)
-        c_bf = tiles("c_bf", 4, [P, QUARTER * PACK], BF16)
-        x_bf = tiles("x_bf", 4, [P, QUARTER * PACK], BF16)
-        c_codes = tiles("c_codes", 4, [P, QUARTER], U32)
-        c_plane = tiles("c_plane", 4, [P, QUARTER], U8)
-        x_codes = tiles("x_codes", 4, [P, QUARTER], U32)
-        x_plane = tiles("x_plane", 4, [P, QUARTER], U8)
-        kc_f32 = tiles("kc_f32", 2, [P, PACK, HALF], F32)
-        kc_bf = tiles("kc_bf", 4, [P, QUARTER * PACK], BF16)
-        kc_codes = sb.tile([P, J], U32, align_bytes=64)
-        kc_plane = sb.tile([P, J], U8, align_bytes=64)
-        qr_bf = tiles("qr_bf", 4, [P, QUARTER * PACK], BF16)
-        qr_codes = tiles("qr_codes", 4, [P, QUARTER], U32)
-        qr_plane = tiles("qr_plane", 4, [P, QUARTER], U8)
-        scores = tiles("scores", 4, [P, J], F32)
-        kc_ps = {}
-        qr_ps = {}
-        sc_ps = {}
+        wk_raw = tile("wk_raw", [P, D // 2], I32)
+        w8_raw = tile("w8_raw", [P, D], I32)
+        scales_raw = tile("scales_raw", [P, 2 * D], U8)
+        wk_codes = tile("wk_codes", [P, 2 * D], U8)
+        w8_codes = tile("w8_codes", [P, D], I32)
+        w_plane = {"wk": tile("wk_plane", [P, D], U8), "w8": tile("w8_plane", [P, D], U8)}
+        w_scales = {"wk": (wk_scales, 0), "w8": (w8_scales, D)}
+        acts = {"c": c, "x": x}
+        kc_f32 = [tile("kc_f32_%d" % h, [P, PACK, HALF], F32) for h in range(2)]
+        raw = {("kc", q): kc_f32[q // 2][:, :, (q % 2) * QUARTER : (q % 2 + 1) * QUARTER] for q in range(4)}
+        raw_piece = {("kc", q): (kc_f32[q // 2], (q // 2) * HALF) for q in range(4)}
+        bf = {name: tile(name + "_bf", [P, PACK * M], BF16) for name in ("c", "x", "kc", "qr")}
+        codes = {name: tile(name + "_codes", [P, M], U32) for name in ("c", "x", "kc", "qr")}
+        plane = {name: tile(name + "_plane", [P, M], U8) for name in ("c", "x", "kc", "qr")}
+        scores = [tile("scores%d" % q, [P, J], F32) for q in range(4)]
+        acc = {}
 
-        def load_scale_rows(dram, col0):
+        def zero_scales():
+            nc.vector.memset(scales_raw[:].bitcast(I32), 0)
+
+        def load_wk():
+            nc.sync.dma_start(out=wk_raw[:], in_=wk_words[0].bitcast(I32))
+
+        def load_w8():
+            nc.sync.dma_start(out=w8_raw[:], in_=w8_words[0].rearrange("p n t -> p (n t)").bitcast(I32))
+
+        def load_scales(name, eng="sync", quadrants=range(4)):
+            dram, col0 = w_scales[name]
             rows = dram[0].bitcast(I32)
-            for q in range(4):
-                nc.sync.dma_start(
+            for q in quadrants:
+                queue[eng].dma_start(
                     out=scales_raw[32 * q : 32 * q + 4, col0 : col0 + D].bitcast(I32),
                     in_=rows[4 * q : 4 * q + 4, :],
                 )
 
-        def load_half(raw, dram, h):
-            view = dram.rearrange("(p t) n -> p t n", t=PACK)
-            nc.sync.dma_start(out=raw[h][:], in_=view[:, :, h * HALF : (h + 1) * HALF])
+        def load(name, col0, width):
+            piece = tile("%s_raw%d" % (name, col0), [P, PACK, width], F32)
+            view = acts[name].rearrange("(p t) n -> p t n", t=PACK)
+            nc.sync.dma_start(out=piece[:], in_=view[:, :, col0 : col0 + width])
+            for q in range(col0 // QUARTER, (col0 + width) // QUARTER):
+                raw_piece[name, q] = (piece, col0)
 
-        def deal_plane(plane, col0):
+        def deal_wk():
             nc.vector.tensor_copy(
-                out=plane[:].rearrange("p (t g i) -> p g t i", t=PACK, i=16),
+                out=wk_codes[:].bitcast(U16).rearrange("p (t g i) -> p g t i", t=PACK, i=8),
+                in_=wk_raw[:].bitcast(U16).rearrange("p (g i t) -> p g t i", t=PACK, i=8),
+            )
+
+        def deal_w8():
+            nc.vector.tensor_copy(
+                out=w8_codes[:].rearrange("p (t g i) -> p g t i", t=PACK, i=4),
+                in_=w8_raw[:].rearrange("p (g i t) -> p g t i", t=PACK, i=4),
+            )
+
+        def deal_plane(name):
+            col0 = w_scales[name][1]
+            nc.vector.tensor_copy(
+                out=w_plane[name][:].rearrange("p (t g i) -> p g t i", t=PACK, i=16),
                 in_=scales_raw[:, col0 : col0 + D].rearrange("p (g i t) -> p g t i", t=PACK, i=16),
             )
 
-        def interleave(engine, dst, src):
-            out = dst.rearrange("p (g i t) -> p g t i", t=PACK, i=2)
-            in_ = src.rearrange("p t (g i) -> p g t i", i=2)
-            if engine == "vector":
+        def round_cols(eng, name, col0, width):
+            piece, base = raw_piece[name, col0 // QUARTER]
+            out = bf[name][:, PACK * col0 : PACK * (col0 + width)].rearrange("p (g i t) -> p g t i", t=PACK, i=2)
+            in_ = piece[:, :, col0 - base : col0 - base + width].rearrange("p t (g i) -> p g t i", i=2)
+            if eng == "vector":
                 nc.vector.tensor_copy(out=out, in_=in_)
             else:
                 nc.scalar.activation(out=out, in_=in_, func=ACT.Copy)
 
-        def round_quarter(engine, bf, raw, q):
-            cols = slice((q % 2) * QUARTER, (q % 2 + 1) * QUARTER)
-            interleave(engine, bf[q][:], raw[q // 2][:, :, cols])
+        def quantize(name, col0, width):
+            nc.vector.quantize_mx(
+                out=codes[name][:, col0 : col0 + width].bitcast(FP8X4),
+                scales=plane[name][:, col0 : col0 + width],
+                in_=bf[name][:, PACK * col0 : PACK * (col0 + width)],
+            )
 
-        def quantize(codes, plane, bf):
-            nc.vector.quantize_mx(out=codes.bitcast(FP8X4), scales=plane, in_=bf)
-
-        def project_keys(q):
-            kc_ps[q] = ps.tile([P, PACK, QUARTER], F32, name="bank_a%d" % q)
+        def project(name, q):
+            cols = slice(q * QUARTER, (q + 1) * QUARTER)
+            result = {"c": "kc", "x": "qr"}[name]
+            acc[result, q] = ps.tile([P, PACK, QUARTER], F32, name="bank%d" % (q if name == "c" else 4 + q))
             for t in range(PACK):
+                if name == "c":
+                    lhsT = wk_codes[:, 2 * P * t : 2 * P * (t + 1)].bitcast(FP4X4)
+                    lhsT_scale = w_plane["wk"][:, P * t : P * (t + 1)]
+                else:
+                    lhsT = w8_codes[:, P * t : P * (t + 1)].bitcast(FP8X4)
+                    lhsT_scale = w_plane["w8"][:, P * t : P * (t + 1)]
                 nc.tensor.matmul_mx(
-                    out=kc_ps[q][:, t, :],
-                    lhsT=wk_codes[:, 2 * P * t : 2 * P * (t + 1)].bitcast(FP4X4),
-                    lhsT_scale=wk_plane[:, P * t : P * (t + 1)],
-                    rhs=c_codes[q][:].bitcast(FP8X4),
-                    rhs_scale=c_plane[q][:],
+                    out=acc[result, q][:, t, :],
+                    lhsT=lhsT,
+                    lhsT_scale=lhsT_scale,
+                    rhs=codes[name][:, cols].bitcast(FP8X4),
+                    rhs_scale=plane[name][:, cols],
                     start=True,
                     stop=True,
                 )
 
-        def project_queries(q):
-            qr_ps[q] = ps.tile([P, PACK, QUARTER], F32, name="bank_b%d" % q)
-            for t in range(PACK):
-                nc.tensor.matmul_mx(
-                    out=qr_ps[q][:, t, :],
-                    lhsT=w8_codes[:, P * t : P * (t + 1)].bitcast(FP8X4),
-                    lhsT_scale=w8_plane[:, P * t : P * (t + 1)],
-                    rhs=x_codes[q][:].bitcast(FP8X4),
-                    rhs_scale=x_plane[q][:],
-                    start=True,
-                    stop=True,
-                )
-
-        def score(q):
-            sc_ps[q] = ps.tile([P, J], F32, name="bank_a%d" % q)
+        def score(q, col0=0, width=J, b=None):
+            rows = slice(q * QUARTER, (q + 1) * QUARTER)
+            cols = slice(col0, col0 + width)
+            acc["sc", q, col0] = ps.tile([P, width], F32, name="bank%d" % (q if b is None else b))
             nc.tensor.matmul_mx(
-                out=sc_ps[q][:],
-                lhsT=qr_codes[q][:].bitcast(FP8X4),
-                lhsT_scale=qr_plane[q][:],
-                rhs=kc_codes[:].bitcast(FP8X4),
-                rhs_scale=kc_plane[:],
+                out=acc["sc", q, col0][:],
+                lhsT=codes["qr"][:, rows].bitcast(FP8X4),
+                lhsT_scale=plane["qr"][:, rows],
+                rhs=codes["kc"][:, cols].bitcast(FP8X4),
+                rhs_scale=plane["kc"][:, cols],
                 start=True,
                 stop=True,
             )
 
-        def drain_keys(q):
-            cols = slice((q % 2) * QUARTER, (q % 2 + 1) * QUARTER)
-            nc.scalar.copy(out=kc_f32[q // 2][:, :, cols], in_=kc_ps[q][:])
+        def drain_keys(eng, q):
+            if eng == "vector":
+                nc.vector.tensor_copy(out=raw["kc", q], in_=acc["kc", q][:])
+            else:
+                nc.scalar.copy(out=raw["kc", q], in_=acc["kc", q][:])
 
-        def drain_queries(engine, q):
-            out = qr_bf[q][:].rearrange("p (n t) -> p n t", t=PACK)
-            in_ = qr_ps[q][:].rearrange("p t n -> p n t")
-            if engine == "vector":
+        def drain_round(eng, name, q):
+            out = bf[name][:, PACK * QUARTER * q : PACK * QUARTER * (q + 1)].rearrange("p (n t) -> p n t", t=PACK)
+            in_ = acc[name, q][:].rearrange("p t n -> p n t")
+            if eng == "vector":
                 nc.vector.tensor_copy(out=out, in_=in_)
             else:
                 nc.scalar.copy(out=out, in_=in_)
 
-        def drain_scores(engine, q):
-            if engine == "vector":
+        def drain_scores(eng, q, col0=0, width=J):
+            out = scores[q][:, col0 : col0 + width]
+            if eng == "vector":
                 nc.vector.tensor_scalar(
-                    out=scores[q][:], in0=sc_ps[q][:], scalar1=0.0, scalar2=SCORE_SCALE, op0=ALU.max, op1=ALU.mult
+                    out=out, in0=acc["sc", q, col0][:], scalar1=0.0, scalar2=SCORE_SCALE, op0=ALU.max, op1=ALU.mult
                 )
             else:
-                nc.scalar.activation(out=scores[q][:], in_=sc_ps[q][:], func=ACT.Relu, scale=SCORE_SCALE)
+                nc.scalar.activation(out=out, in_=acc["sc", q, col0][:], func=ACT.Relu, scale=SCORE_SCALE)
 
-        def store_scores(q):
-            nc.sync.dma_start(out=out_0[q * QUARTER : (q + 1) * QUARTER, :], in_=scores[q][:])
+        def store_scores(q, col0=0, width=J, eng="sync"):
+            queue[eng].dma_start(
+                out=out_0[q * QUARTER : (q + 1) * QUARTER, col0 : col0 + width], in_=scores[q][:, col0 : col0 + width]
+            )
 
-        def store_keys(h):
+        def store_keys(col0, width):
             view = out_1.rearrange("(p t) n -> p t n", t=PACK)
-            nc.sync.dma_start(out=view[:, :, h * HALF : (h + 1) * HALF], in_=kc_f32[h][:])
+            piece, base = raw_piece["kc", col0 // QUARTER]
+            nc.sync.dma_start(out=view[:, :, col0 : col0 + width], in_=piece[:, :, col0 - base : col0 - base + width])
 
-        def quantize_keys(q):
-            cols = slice(q * QUARTER, (q + 1) * QUARTER)
-            quantize(kc_codes[:, cols], kc_plane[:, cols], kc_bf[q][:])
+        def store_codes(col0=0, width=J):
+            words = out_2[0].rearrange("p n t -> p (n t)").bitcast(I32)
+            nc.sync.dma_start(out=words[:, col0 : col0 + width], in_=codes["kc"][:, col0 : col0 + width].bitcast(I32))
 
-        nc.vector.memset(scales_raw[:].bitcast(I32), 0)
-        nc.sync.dma_start(out=wk_raw[:].bitcast(I32), in_=wk_words[0].bitcast(I32))
-        load_half(c_raw, c, 0)
-        load_scale_rows(wk_scales, 0)
-        load_half(c_raw, c, 1)
-        nc.sync.dma_start(out=w8_raw[:], in_=w8_words[0].rearrange("p n t -> p (n t)").bitcast(I32))
-        load_scale_rows(w8_scales, D)
-        load_half(x_raw, x, 0)
-        load_half(x_raw, x, 1)
-        nc.vector.tensor_copy(
-            out=wk_codes[:].rearrange("p (t g i b) -> p g t i b", t=PACK, i=8, b=2),
-            in_=wk_raw[:].rearrange("p (g i t b) -> p g t i b", t=PACK, i=8, b=2),
-        )
-        round_quarter("vector", c_bf, c_raw, 0)
-        round_quarter("scalar", c_bf, c_raw, 1)
-        deal_plane(wk_plane, 0)
-        quantize(c_codes[0][:], c_plane[0][:], c_bf[0][:])
-        project_keys(0)
-        quantize(c_codes[1][:], c_plane[1][:], c_bf[1][:])
-        project_keys(1)
-        round_quarter("vector", c_bf, c_raw, 2)
-        round_quarter("scalar", c_bf, c_raw, 3)
-        quantize(c_codes[2][:], c_plane[2][:], c_bf[2][:])
-        project_keys(2)
-        drain_keys(0)
-        nc.vector.tensor_copy(
-            out=w8_codes[:].rearrange("p (t g i) -> p g t i", t=PACK, i=4),
-            in_=w8_raw[:].rearrange("p (g i t) -> p g t i", t=PACK, i=4),
-        )
-        quantize(c_codes[3][:], c_plane[3][:], c_bf[3][:])
-        project_keys(3)
-        drain_keys(1)
-        deal_plane(w8_plane, D)
-        round_quarter("vector", kc_bf, kc_f32, 0)
-        drain_keys(2)
-        store_keys(0)
-        drain_keys(3)
-        store_keys(1)
-        round_quarter("vector", x_bf, x_raw, 0)
-        round_quarter("vector", x_bf, x_raw, 1)
-        quantize(x_codes[0][:], x_plane[0][:], x_bf[0][:])
-        project_queries(0)
-        quantize(x_codes[1][:], x_plane[1][:], x_bf[1][:])
-        project_queries(1)
-        round_quarter("scalar", kc_bf, kc_f32, 2)
-        round_quarter("scalar", kc_bf, kc_f32, 3)
-        round_quarter("vector", kc_bf, kc_f32, 1)
-        round_quarter("vector", x_bf, x_raw, 2)
-        quantize_keys(0)
-        round_quarter("vector", x_bf, x_raw, 3)
-        quantize(x_codes[2][:], x_plane[2][:], x_bf[2][:])
-        project_queries(2)
-        quantize_keys(1)
-        quantize(x_codes[3][:], x_plane[3][:], x_bf[3][:])
-        project_queries(3)
-        quantize_keys(2)
-        quantize_keys(3)
-        nc.sync.dma_start(out=out_2[0].rearrange("p n t -> p (n t)").bitcast(I32), in_=kc_codes[:].bitcast(I32))
+        def store_plane():
+            for q in range(4):
+                nc.sync.dma_start(
+                    out=out_3[0].bitcast(I32)[4 * q : 4 * q + 4, :], in_=plane["kc"][32 * q : 32 * q + 4, :].bitcast(I32)
+                )
+
+        V, S, Q = "vector", "scalar", QUARTER
+        zero_scales()
+        load_wk()
+        load("c", 0, Q)
+        load_scales("wk")
+        for q in range(1, 4):
+            load("c", q * Q, Q)
+        load_w8()
+        load("x", 0, Q)
+        load_scales("w8")
+        for q in range(1, 4):
+            load("x", q * Q, Q)
+
+        def empty_keys(q):
+            if q < 3:
+                drain_round(S, "kc", q)
+            drain_keys(S, q)
+            if q % 2 == 1:
+                store_keys((q - 1) * Q, HALF)
+
+        deal_wk()
+        round_cols(V, "c", 0, Q)
+        deal_plane("wk")
         for q in range(4):
-            nc.sync.dma_start(out=out_3[0].bitcast(I32)[4 * q : 4 * q + 4, :], in_=kc_plane[32 * q : 32 * q + 4, :].bitcast(I32))
-        drain_queries("scalar", 0)
-        drain_queries("scalar", 1)
-        quantize(qr_codes[0][:], qr_plane[0][:], qr_bf[0][:])
+            if 0 < q < 3:
+                round_cols(V, "c", (q + 1) * Q, Q)
+            quantize("c", q * Q, Q)
+            project("c", q)
+            if q == 0:
+                round_cols(S, "c", Q, Q)
+        for q in range(4):
+            empty_keys(q)
+        deal_w8()
+        for q in range(4):
+            round_cols(V, "x", q * Q, Q)
+            if q == 0:
+                deal_plane("w8")
+            else:
+                quantize("kc", (q - 1) * Q, Q)
+            quantize("x", q * Q, Q)
+            project("x", q)
+        round_cols(V, "kc", 3 * Q, Q)
+        drain_round(S, "qr", 0)
+        quantize("qr", 0, Q)
+        quantize("kc", 3 * Q, Q)
         score(0)
-        quantize(qr_codes[1][:], qr_plane[1][:], qr_bf[1][:])
+        store_codes()
+        store_plane()
+
+        drain_round(S, "qr", 1)
+        quantize("qr", Q, Q)
         score(1)
-        drain_queries("scalar", 2)
-        drain_queries("vector", 3)
-        drain_scores("scalar", 0)
-        store_scores(0)
-        quantize(qr_codes[2][:], qr_plane[2][:], qr_bf[2][:])
-        score(2)
-        quantize(qr_codes[3][:], qr_plane[3][:], qr_bf[3][:])
-        score(3)
-        drain_scores("vector", 1)
-        store_scores(1)
-        drain_scores("scalar", 2)
-        store_scores(2)
-        drain_scores("vector", 3)
-        store_scores(3)
+        drain_round(S, "qr", 2)
+        drain_round(V, "qr", 3)
+        for q in (2, 3):
+            quantize("qr", q * Q, Q)
+            score(q)
+        for q in range(4):
+            drain_scores(S if q % 2 == 0 else V, q)
+            store_scores(q)

@@ -204,25 +204,31 @@ def tile_mix_kvw_relu_kernel(
         for q in range(1, 4):
             load("x", q * Q, Q)
 
-        def empty_keys(q):
-            if q < 3:
+        def round_shared(name, q):
+            round_cols(V, name, q * Q, Q // 2)
+            round_cols(S, name, q * Q + Q // 2, Q // 2)
+
+        deal_wk()
+        round_shared("c", 0)
+        deal_plane("wk")
+        quantize("c", 0, Q)
+        project("c", 0)
+        for q in (1, 2):
+            round_shared("c", q)
+            quantize("c", q * Q, Q)
+            project("c", q)
+        drain_keys(S, 0)
+        round_cols(V, "c", 3 * Q, Q)
+        round_cols(V, "kc", 0, Q)
+        quantize("c", 3 * Q, Q)
+        project("c", 3)
+        for q in (1, 2, 3):
+            if q in (1, 2):
                 drain_round(S, "kc", q)
             drain_keys(S, q)
             if q % 2 == 1:
                 store_keys((q - 1) * Q, HALF)
 
-        deal_wk()
-        round_cols(V, "c", 0, Q)
-        deal_plane("wk")
-        for q in range(4):
-            if 0 < q < 3:
-                round_cols(V, "c", (q + 1) * Q, Q)
-            quantize("c", q * Q, Q)
-            project("c", q)
-            if q == 0:
-                round_cols(S, "c", Q, Q)
-        for q in range(4):
-            empty_keys(q)
         deal_w8()
         for q in range(4):
             round_cols(V, "x", q * Q, Q)
@@ -232,22 +238,32 @@ def tile_mix_kvw_relu_kernel(
                 quantize("kc", (q - 1) * Q, Q)
             quantize("x", q * Q, Q)
             project("x", q)
+
+        def score_tile(q):
+            for h in range(2):
+                score(q, h * HALF, HALF, 2 * q + h)
+
+        def finish(q, engines):
+            for h in range(2):
+                drain_scores(engines[h], q, h * HALF, HALF)
+            store_scores(q)
+
+        for q in range(4):
+            drain_round(S, "qr", q)
         round_cols(V, "kc", 3 * Q, Q)
-        drain_round(S, "qr", 0)
         quantize("qr", 0, Q)
         quantize("kc", 3 * Q, Q)
-        score(0)
+        score_tile(0)
         store_codes()
-        store_plane()
-
-        drain_round(S, "qr", 1)
-        quantize("qr", Q, Q)
-        score(1)
-        drain_round(S, "qr", 2)
-        drain_round(V, "qr", 3)
-        for q in (2, 3):
+        for q in (1, 2):
             quantize("qr", q * Q, Q)
-            score(q)
-        for q in range(4):
-            drain_scores(S if q % 2 == 0 else V, q)
-            store_scores(q)
+            score_tile(q)
+        drain_scores(V, 0, 0, HALF)
+        store_scores(0, 0, HALF)
+        quantize("qr", 3 * Q, Q)
+        score_tile(3)
+        drain_scores(S, 0, HALF, HALF)
+        store_scores(0, HALF, HALF)
+        for q in (1, 2, 3):
+            finish(q, (V, S))
+        store_plane()

@@ -67,14 +67,14 @@ def tile_mix_kvw_relu_kernel(
             rows = dram[0].bitcast(I32)
             for q in quadrants:
                 queue[eng].dma_start(
-                    out=scales_raw[32 * q : 32 * q + 4, col0 : col0 + D].bitcast(I32),
-                    in_=rows[4 * q : 4 * q + 4, :],
+                    out=scales_raw[q:P:32, col0 : col0 + D].bitcast(I32),
+                    in_=rows[q:16:4, :],
                 )
 
-        def load(name, col0, width):
+        def load(name, col0, width, eng="sync"):
             piece = tile("%s_raw%d" % (name, col0), [P, PACK, width], F32)
             view = acts[name].rearrange("(p t) n -> p t n", t=PACK)
-            nc.sync.dma_start(out=piece[:], in_=view[:, :, col0 : col0 + width])
+            queue[eng].dma_start(out=piece[:], in_=view[:, :, col0 : col0 + width])
             for q in range(col0 // QUARTER, (col0 + width) // QUARTER):
                 raw_piece[name, q] = (piece, col0)
 
@@ -188,7 +188,7 @@ def tile_mix_kvw_relu_kernel(
         def store_plane():
             for q in range(4):
                 nc.sync.dma_start(
-                    out=out_3[0].bitcast(I32)[4 * q : 4 * q + 4, :], in_=plane["kc"][32 * q : 32 * q + 4, :].bitcast(I32)
+                    out=out_3[0].bitcast(I32)[q:16:4, :], in_=plane["kc"][q:P:32, :].bitcast(I32)
                 )
 
         V, S, Q = "vector", "scalar", QUARTER
@@ -255,15 +255,14 @@ def tile_mix_kvw_relu_kernel(
         quantize("kc", 3 * Q, Q)
         score_tile(0)
         store_codes()
+        store_plane()
         for q in (1, 2):
             quantize("qr", q * Q, Q)
             score_tile(q)
         drain_scores(V, 0, 0, HALF)
-        store_scores(0, 0, HALF)
         quantize("qr", 3 * Q, Q)
         score_tile(3)
         drain_scores(S, 0, HALF, HALF)
-        store_scores(0, HALF, HALF)
+        store_scores(0)
         for q in (1, 2, 3):
             finish(q, (V, S))
-        store_plane()

@@ -185,9 +185,9 @@ def tile_mix_kvw_relu_kernel(
             words = out_2[0].rearrange("p n t -> p (n t)").bitcast(I32)
             nc.sync.dma_start(out=words[:, col0 : col0 + width], in_=codes["kc"][:, col0 : col0 + width].bitcast(I32))
 
-        def store_plane():
+        def store_plane(eng="sync"):
             for q in range(4):
-                nc.sync.dma_start(
+                queue[eng].dma_start(
                     out=out_3[0].bitcast(I32)[q:16:4, :], in_=plane["kc"][q:P:32, :].bitcast(I32)
                 )
 
@@ -234,8 +234,13 @@ def tile_mix_kvw_relu_kernel(
             round_cols(V, "x", q * Q, Q)
             if q == 0:
                 deal_plane("w8")
+            elif q == 1:
+                quantize("kc", 0, HALF)
+            elif q == 2:
+                quantize("kc", 2 * Q, Q)
+                store_codes(0, HALF)
             else:
-                quantize("kc", (q - 1) * Q, Q)
+                round_cols(V, "kc", 3 * Q, Q)
             quantize("x", q * Q, Q)
             project("x", q)
 
@@ -250,11 +255,10 @@ def tile_mix_kvw_relu_kernel(
 
         for q in range(4):
             drain_round(S, "qr", q)
-        round_cols(V, "kc", 3 * Q, Q)
-        quantize("qr", 0, Q)
         quantize("kc", 3 * Q, Q)
+        quantize("qr", 0, Q)
         score_tile(0)
-        store_codes()
+        store_codes(HALF, HALF)
         store_plane()
         for q in (1, 2):
             quantize("qr", q * Q, Q)

@@ -78,8 +78,9 @@ def tile_mix_kvw_relu_kernel(
             for q in range(col0 // QUARTER, (col0 + width) // QUARTER):
                 raw_piece[name, q] = (piece, col0)
 
-        def deal_wk():
-            nc.vector.tensor_copy(
+        def deal_wk(eng="vector"):
+            copy = nc.vector.tensor_copy if eng == "vector" else nc.scalar.copy
+            copy(
                 out=wk_codes[:].bitcast(U16).rearrange("p (t g i) -> p g t i", t=PACK, i=8),
                 in_=wk_raw[:].bitcast(U16).rearrange("p (g i t) -> p g t i", t=PACK, i=8),
             )
@@ -113,10 +114,11 @@ def tile_mix_kvw_relu_kernel(
                 in_=bf[name][:, PACK * col0 : PACK * (col0 + width)],
             )
 
-        def project(name, q):
+        def project(name, q, b=None):
             cols = slice(q * QUARTER, (q + 1) * QUARTER)
             result = {"c": "kc", "x": "qr"}[name]
-            acc[result, q] = ps.tile([P, PACK, QUARTER], F32, name="bank%d" % (q if name == "c" else 4 + q))
+            home = q if name == "c" else 4 + q
+            acc[result, q] = ps.tile([P, PACK, QUARTER], F32, name="bank%d" % (home if b is None else b))
             for t in range(PACK):
                 if name == "c":
                     lhsT = wk_codes[:, 2 * P * t : 2 * P * (t + 1)].bitcast(FP4X4)
@@ -192,81 +194,110 @@ def tile_mix_kvw_relu_kernel(
                 )
 
         V, S, Q = "vector", "scalar", QUARTER
-        zero_scales()
-        load_wk()
-        load("c", 0, Q)
-        load_scales("wk")
-        for q in range(1, 4):
-            load("c", q * Q, Q)
-        load_w8()
-        load("x", 0, Q)
-        load_scales("w8")
-        for q in range(1, 4):
-            load("x", q * Q, Q)
 
         def round_shared(name, q):
             round_cols(V, name, q * Q, Q // 2)
             round_cols(S, name, q * Q + Q // 2, Q // 2)
 
-        deal_wk()
-        round_shared("c", 0)
-        deal_plane("wk")
-        quantize("c", 0, Q)
-        project("c", 0)
-        for q in (1, 2):
-            round_shared("c", q)
-            quantize("c", q * Q, Q)
-            project("c", q)
-        drain_keys(S, 0)
-        round_cols(V, "c", 3 * Q, Q)
-        round_cols(V, "kc", 0, Q)
-        quantize("c", 3 * Q, Q)
-        project("c", 3)
-        for q in (1, 2, 3):
-            if q in (1, 2):
-                drain_round(S, "kc", q)
-            drain_keys(S, q)
-            if q % 2 == 1:
-                store_keys((q - 1) * Q, HALF)
-
-        deal_w8()
-        for q in range(4):
-            round_cols(V, "x", q * Q, Q)
-            if q == 0:
-                deal_plane("w8")
-            elif q == 1:
-                quantize("kc", 0, HALF)
-            elif q == 2:
-                quantize("kc", 2 * Q, Q)
-                store_codes(0, HALF)
-            else:
-                round_cols(V, "kc", 3 * Q, Q)
-            quantize("x", q * Q, Q)
-            project("x", q)
-
         def score_tile(q):
-            for h in range(2):
-                score(q, h * HALF, HALF, 2 * q + h)
+            score(q, 0, HALF, 4 + q)
+            score(q, HALF, HALF, q)
 
         def finish(q, engines):
             for h in range(2):
                 drain_scores(engines[h], q, h * HALF, HALF)
             store_scores(q)
 
-        for q in range(4):
-            drain_round(S, "qr", q)
-        quantize("kc", 3 * Q, Q)
+
+        def warm_up(passes):
+            zeros = tile("warm_bf", [P, PACK * J], BF16)
+            warm_codes = tile("warm_codes", [P, J], U32)
+            warm_plane = tile("warm_plane", [P, J], U8)
+            nc.gpsimd.memset(zeros[:].bitcast(I32), 0)
+            nc.vector.quantize_mx(out=warm_codes[:].bitcast(FP8X4), scales=warm_plane[:], in_=zeros[:])
+            bank = ps.tile([P, J], F32, name="bank7")
+            for n in range(passes):
+                nc.tensor.matmul_mx(
+                    out=bank[:],
+                    lhsT=warm_codes[:, :P].bitcast(FP8X4),
+                    lhsT_scale=warm_plane[:, :P],
+                    rhs=warm_codes[:].bitcast(FP8X4),
+                    rhs_scale=warm_plane[:],
+                    start=(n == 0),
+                    stop=(n == passes - 1),
+                )
+
+        zero_scales()
+        load_wk()
+        load("c", 0, Q)
+        load_scales("wk")
+        for q in range(1, 4):
+            load("c", q * Q, Q)
+        load("x", 0, Q)
+        load_scales("w8")
+        load_w8()
+        for q in range(1, 4):
+            load("x", q * Q, Q)
+
+        warm_up(3)
+        deal_wk()
+        round_shared("c", 0)
+        deal_plane("wk")
+        quantize("c", 0, Q)
+        project("c", 0)
+        round_shared("c", 1)
+        quantize("c", Q, Q)
+        project("c", 1)
+        round_cols(V, "c", 2 * Q, Q)
+        round_cols(V, "c", 3 * Q, Q)
+        quantize("c", 2 * Q, Q)
+        project("c", 2)
+        round_cols(V, "x", 0, Q)
+        quantize("c", 3 * Q, Q)
+        project("c", 3)
+        deal_plane("w8")
+        quantize("x", 0, Q)
+        deal_w8()
+        project("x", 0)
+        drain_round(S, "kc", 0)
+        drain_keys(S, 0)
+        drain_keys(S, 1)
+        store_keys(0, HALF)
+        drain_round(S, "kc", 2)
+        drain_keys(S, 2)
+        store_keys(HALF, Q)
+        drain_round(S, "kc", 3)
+        drain_round(S, "qr", 0)
+        drain_keys(S, 3)
+        round_cols(V, "kc", Q, Q)
+        round_cols(V, "x", Q, Q)
+        quantize("kc", 0, HALF)
+        quantize("x", Q, Q)
+        project("x", 1)
+        drain_round(S, "qr", 1)
+        round_cols(V, "x", 2 * Q, Q)
+        quantize("kc", HALF, HALF)
+        store_codes()
+        store_plane()
+        store_keys(3 * Q, Q)
+        quantize("x", 2 * Q, Q)
+        project("x", 2)
+        drain_round(S, "qr", 2)
+        round_cols(V, "x", 3 * Q, Q)
         quantize("qr", 0, Q)
         score_tile(0)
-        store_codes(HALF, HALF)
-        store_plane()
-        for q in (1, 2):
-            quantize("qr", q * Q, Q)
-            score_tile(q)
-        drain_scores(V, 0, 0, HALF)
+        quantize("x", 3 * Q, Q)
+        project("x", 3)
+        drain_round(S, "qr", 3)
+        quantize("qr", Q, Q)
+        score_tile(1)
+        finish(0, (V, V))
+        quantize("qr", 2 * Q, Q)
+        score_tile(2)
+        drain_scores(V, 1, 0, HALF)
         quantize("qr", 3 * Q, Q)
         score_tile(3)
-        drain_scores(S, 0, HALF, HALF)
-        store_scores(0)
-        for q in (1, 2, 3):
-            finish(q, (V, S))
+        drain_scores(S, 1, HALF, HALF)
+        store_scores(1)
+        finish(2, (V, S))
+        finish(3, (V, S))

@@ -18,6 +18,7 @@ ALU = mybir.AluOpType
 
 P = 128
 PACK = 4
+EIGHTH = 64
 QUARTER = 128
 HALF = 256
 SCORE_SCALE = 0.03125
@@ -46,7 +47,7 @@ def tile_mix_kvw_relu_kernel(
         acts = {"c": c, "x": x}
         kc_f32 = [tile("kc_f32_%d" % h, [P, PACK, HALF], F32) for h in range(2)]
         raw = {("kc", q): kc_f32[q // 2][:, :, (q % 2) * QUARTER : (q % 2 + 1) * QUARTER] for q in range(4)}
-        raw_piece = {("kc", q): (kc_f32[q // 2], (q // 2) * HALF) for q in range(4)}
+        raw_piece = {("kc", e): (kc_f32[e // 4], (e // 4) * HALF) for e in range(8)}
         bf = {name: tile(name + "_bf", [P, PACK * M], BF16) for name in ("c", "x", "kc", "qr")}
         codes = {name: tile(name + "_codes", [P, M], U32) for name in ("c", "x", "kc", "qr")}
         plane = {name: tile(name + "_plane", [P, M], U8) for name in ("c", "x", "kc", "qr")}
@@ -75,8 +76,8 @@ def tile_mix_kvw_relu_kernel(
             piece = tile("%s_raw%d" % (name, col0), [P, PACK, width], F32)
             view = acts[name].rearrange("(p t) n -> p t n", t=PACK)
             queue[eng].dma_start(out=piece[:], in_=view[:, :, col0 : col0 + width])
-            for q in range(col0 // QUARTER, (col0 + width) // QUARTER):
-                raw_piece[name, q] = (piece, col0)
+            for e in range(col0 // EIGHTH, (col0 + width) // EIGHTH):
+                raw_piece[name, e] = (piece, col0)
 
         def deal_wk(eng="vector"):
             copy = nc.vector.tensor_copy if eng == "vector" else nc.scalar.copy
@@ -91,15 +92,15 @@ def tile_mix_kvw_relu_kernel(
                 in_=w8_raw[:].rearrange("p (g i t) -> p g t i", t=PACK, i=4),
             )
 
-        def deal_plane(name):
+        def deal_plane(name, t0=0, t1=PACK):
             col0 = w_scales[name][1]
             nc.vector.tensor_copy(
-                out=w_plane[name][:].rearrange("p (t g i) -> p g t i", t=PACK, i=16),
-                in_=scales_raw[:, col0 : col0 + D].rearrange("p (g i t) -> p g t i", t=PACK, i=16),
+                out=w_plane[name][:].rearrange("p (t g i) -> p g t i", t=PACK, i=16)[:, :, t0:t1, :],
+                in_=scales_raw[:, col0 : col0 + D].rearrange("p (g i t) -> p g t i", t=PACK, i=16)[:, :, t0:t1, :],
             )
 
         def round_cols(eng, name, col0, width):
-            piece, base = raw_piece[name, col0 // QUARTER]
+            piece, base = raw_piece[name, col0 // EIGHTH]
             out = bf[name][:, PACK * col0 : PACK * (col0 + width)].rearrange("p (g i t) -> p g t i", t=PACK, i=2)
             in_ = piece[:, :, col0 - base : col0 - base + width].rearrange("p t (g i) -> p g t i", i=2)
             if eng == "vector":
@@ -135,6 +136,28 @@ def tile_mix_kvw_relu_kernel(
                     start=True,
                     stop=True,
                 )
+
+        def project_part(col0, width, b):
+            cols = slice(col0, col0 + width)
+            acc["qr", col0, width] = ps.tile([P, PACK, width], F32, name="bank%d" % b)
+            for t in range(PACK):
+                nc.tensor.matmul_mx(
+                    out=acc["qr", col0, width][:, t, :],
+                    lhsT=w8_codes[:, P * t : P * (t + 1)].bitcast(FP8X4),
+                    lhsT_scale=w_plane["w8"][:, P * t : P * (t + 1)],
+                    rhs=codes["x"][:, cols].bitcast(FP8X4),
+                    rhs_scale=plane["x"][:, cols],
+                    start=True,
+                    stop=True,
+                )
+
+        def drain_part(eng, col0, width):
+            out = bf["qr"][:, PACK * col0 : PACK * (col0 + width)].rearrange("p (n t) -> p n t", t=PACK)
+            in_ = acc["qr", col0, width][:].rearrange("p t n -> p n t")
+            if eng == "vector":
+                nc.vector.tensor_copy(out=out, in_=in_)
+            else:
+                nc.scalar.copy(out=out, in_=in_)
 
         def score(q, col0=0, width=J, b=None):
             rows = slice(q * QUARTER, (q + 1) * QUARTER)
@@ -180,7 +203,7 @@ def tile_mix_kvw_relu_kernel(
 
         def store_keys(col0, width):
             view = out_1.rearrange("(p t) n -> p t n", t=PACK)
-            piece, base = raw_piece["kc", col0 // QUARTER]
+            piece, base = raw_piece["kc", col0 // EIGHTH]
             nc.sync.dma_start(out=view[:, :, col0 : col0 + width], in_=piece[:, :, col0 - base : col0 - base + width])
 
         def store_codes(col0=0, width=J):
@@ -210,11 +233,13 @@ def tile_mix_kvw_relu_kernel(
 
 
         def warm_up(passes):
-            zeros = tile("warm_bf", [P, PACK * J], BF16)
+            zeros = tile("warm_bf", [P, PACK * HALF], BF16)
             warm_codes = tile("warm_codes", [P, J], U32)
             warm_plane = tile("warm_plane", [P, J], U8)
-            nc.gpsimd.memset(zeros[:].bitcast(I32), 0)
-            nc.vector.quantize_mx(out=warm_codes[:].bitcast(FP8X4), scales=warm_plane[:], in_=zeros[:])
+            nc.vector.memset(zeros[:].bitcast(I32), 0)
+            for h in range(2):
+                cols = slice(h * HALF, (h + 1) * HALF)
+                nc.vector.quantize_mx(out=warm_codes[:, cols].bitcast(FP8X4), scales=warm_plane[:, cols], in_=zeros[:])
             bank = ps.tile([P, J], F32, name="bank7")
             for n in range(passes):
                 nc.tensor.matmul_mx(
@@ -249,9 +274,9 @@ def tile_mix_kvw_relu_kernel(
         quantize("c", Q, Q)
         project("c", 1)
         round_cols(V, "c", 2 * Q, Q)
-        round_cols(V, "c", 3 * Q, Q)
         quantize("c", 2 * Q, Q)
         project("c", 2)
+        round_cols(V, "c", 3 * Q, Q)
         round_cols(V, "x", 0, Q)
         quantize("c", 3 * Q, Q)
         project("c", 3)

@@ -232,26 +232,6 @@ def tile_mix_kvw_relu_kernel(
             store_scores(q)
 
 
-        def warm_up(passes):
-            zeros = tile("warm_bf", [P, PACK * HALF], BF16)
-            warm_codes = tile("warm_codes", [P, J], U32)
-            warm_plane = tile("warm_plane", [P, J], U8)
-            nc.vector.memset(zeros[:].bitcast(I32), 0)
-            for h in range(2):
-                cols = slice(h * HALF, (h + 1) * HALF)
-                nc.vector.quantize_mx(out=warm_codes[:, cols].bitcast(FP8X4), scales=warm_plane[:, cols], in_=zeros[:])
-            bank = ps.tile([P, J], F32, name="bank7")
-            for n in range(passes):
-                nc.tensor.matmul_mx(
-                    out=bank[:],
-                    lhsT=warm_codes[:, :P].bitcast(FP8X4),
-                    lhsT_scale=warm_plane[:, :P],
-                    rhs=warm_codes[:].bitcast(FP8X4),
-                    rhs_scale=warm_plane[:],
-                    start=(n == 0),
-                    stop=(n == passes - 1),
-                )
-
         zero_scales()
         load_wk()
         load("c", 0, Q)
@@ -264,7 +244,6 @@ def tile_mix_kvw_relu_kernel(
         for q in range(1, 4):
             load("x", q * Q, Q)
 
-        warm_up(3)
         deal_wk()
         round_shared("c", 0)
         deal_plane("wk")

@@ -101,8 +101,8 @@ def tile_mix_kvw_relu_kernel(
 
         def round_cols(eng, name, col0, width):
             piece, base = raw_piece[name, col0 // EIGHTH]
-            out = bf[name][:, PACK * col0 : PACK * (col0 + width)].rearrange("p (g i t) -> p g t i", t=PACK, i=2)
-            in_ = piece[:, :, col0 - base : col0 - base + width].rearrange("p t (g i) -> p g t i", i=2)
+            out = bf[name][:, PACK * col0 : PACK * (col0 + width)].rearrange("p (g i t) -> p g t i", t=PACK, i=4)
+            in_ = piece[:, :, col0 - base : col0 - base + width].rearrange("p t (g i) -> p g t i", i=4)
             if eng == "vector":
                 nc.vector.tensor_copy(out=out, in_=in_)
             else:

@@ -41,8 +41,9 @@ def tile_mix_kvw_relu_kernel(
         w8_raw = tile("w8_raw", [P, D], I32)
         scales_raw = tile("scales_raw", [P, 2 * D], U8)
         wk_codes = tile("wk_codes", [P, 2 * D], U8)
+        wk_plane = [tile("wk_plane%d" % h, [P, HALF], U8) for h in range(2)]
         w8_codes = tile("w8_codes", [P, D], I32)
-        w_plane = {"wk": tile("wk_plane", [P, D], U8), "w8": tile("w8_plane", [P, D], U8)}
+        w_plane = {"w8": tile("w8_plane", [P, D], U8)}
         w_scales = {"wk": (wk_scales, 0), "w8": (w8_scales, D)}
         acts = {"c": c, "x": x}
         kc_f32 = [tile("kc_f32_%d" % h, [P, PACK, HALF], F32) for h in range(2)]
@@ -79,11 +80,16 @@ def tile_mix_kvw_relu_kernel(
             for e in range(col0 // EIGHTH, (col0 + width) // EIGHTH):
                 raw_piece[name, e] = (piece, col0)
 
-        def deal_wk(eng="vector"):
-            copy = nc.vector.tensor_copy if eng == "vector" else nc.scalar.copy
-            copy(
+        def deal_wk():
+            nc.vector.tensor_copy(
                 out=wk_codes[:].bitcast(U16).rearrange("p (t g i) -> p g t i", t=PACK, i=8),
                 in_=wk_raw[:].bitcast(U16).rearrange("p (g i t) -> p g t i", t=PACK, i=8),
+            )
+
+        def deal_wk_plane(h):
+            nc.vector.tensor_copy(
+                out=wk_plane[h][:].rearrange("p (t g i) -> p g t i", t=2, i=16),
+                in_=scales_raw[:, 0:D].rearrange("p (g i t) -> p g t i", t=PACK, i=16)[:, :, 2 * h : 2 * h + 2, :],
             )
 
         def deal_w8():
@@ -115,15 +121,16 @@ def tile_mix_kvw_relu_kernel(
                 in_=bf[name][:, PACK * col0 : PACK * (col0 + width)],
             )
 
-        def project(name, q, b=None):
+        def project(name, q, t0=0, t1=PACK):
             cols = slice(q * QUARTER, (q + 1) * QUARTER)
             result = {"c": "kc", "x": "qr"}[name]
             home = q if name == "c" else 4 + q
-            acc[result, q] = ps.tile([P, PACK, QUARTER], F32, name="bank%d" % (home if b is None else b))
-            for t in range(PACK):
+            if t0 == 0:
+                acc[result, q] = ps.tile([P, PACK, QUARTER], F32, name="bank%d" % home)
+            for t in range(t0, t1):
                 if name == "c":
                     lhsT = wk_codes[:, 2 * P * t : 2 * P * (t + 1)].bitcast(FP4X4)
-                    lhsT_scale = w_plane["wk"][:, P * t : P * (t + 1)]
+                    lhsT_scale = wk_plane[t // 2][:, P * (t % 2) : P * (t % 2 + 1)]
                 else:
                     lhsT = w8_codes[:, P * t : P * (t + 1)].bitcast(FP8X4)
                     lhsT_scale = w_plane["w8"][:, P * t : P * (t + 1)]
@@ -218,9 +225,9 @@ def tile_mix_kvw_relu_kernel(
 
         V, S, Q = "vector", "scalar", QUARTER
 
-        def round_shared(name, q):
-            round_cols(V, name, q * Q, Q // 2)
-            round_cols(S, name, q * Q + Q // 2, Q // 2)
+        def round_shared(name, q, share=Q // 2):
+            round_cols(V, name, q * Q, share)
+            round_cols(S, name, q * Q + share, Q - share)
 
         def score_tile(q):
             score(q, 0, HALF, 4 + q)
@@ -245,11 +252,13 @@ def tile_mix_kvw_relu_kernel(
             load("x", q * Q, Q)
 
         deal_wk()
-        round_shared("c", 0)
-        deal_plane("wk")
+        round_shared("c", 0, 88)
+        deal_wk_plane(0)
         quantize("c", 0, Q)
-        project("c", 0)
-        round_shared("c", 1)
+        project("c", 0, 0, 2)
+        deal_wk_plane(1)
+        project("c", 0, 2, 4)
+        round_shared("c", 1, 88)
         quantize("c", Q, Q)
         project("c", 1)
         round_cols(V, "c", 2 * Q, Q)
@@ -303,5 +312,5 @@ def tile_mix_kvw_relu_kernel(
         score_tile(3)
         drain_scores(S, 1, HALF, HALF)
         store_scores(1)
-        finish(2, (V, S))
-        finish(3, (V, S))
+        finish(2, (S, V))
+        finish(3, (S, V))

@@ -32,7 +32,7 @@ def tile_mix_kvw_relu_kernel(
         sb = ctx.enter_context(tc.tile_pool(name="sb", bufs=1))
         ps = ctx.enter_context(tc.psum_pool(name="ps", bufs=1))
         ctx.enter_context(tc.manual_schedule())
-        queue = {"sync": nc.sync, "scalar": nc.scalar}
+        queue = {"sync": nc.sync, "scalar": nc.scalar, "gpsimd": nc.gpsimd}
 
         def tile(name, shape, dtype):
             return sb.tile(shape, dtype, name=name, align_bytes=64)
@@ -40,7 +40,9 @@ def tile_mix_kvw_relu_kernel(
         wk_raw = tile("wk_raw", [P, D // 2], I32)
         w8_raw = tile("w8_raw", [P, D], I32)
         scales_raw = tile("scales_raw", [P, 2 * D], U8)
-        wk_codes = tile("wk_codes", [P, 2 * D], U8)
+        wk_codes = [tile("wk_codes%d" % h, [P, D], U8) for h in range(2)]
+        wk_whole = tile("wk_whole", [P, 2 * D], U8)
+        wk_view = {}
         wk_plane = [tile("wk_plane%d" % h, [P, HALF], U8) for h in range(2)]
         w8_codes = tile("w8_codes", [P, D], I32)
         w_plane = {"w8": tile("w8_plane", [P, D], U8)}
@@ -58,11 +60,11 @@ def tile_mix_kvw_relu_kernel(
         def zero_scales():
             nc.vector.memset(scales_raw[:].bitcast(I32), 0)
 
-        def load_wk():
-            nc.sync.dma_start(out=wk_raw[:], in_=wk_words[0].bitcast(I32))
+        def load_wk(eng="sync"):
+            queue[eng].dma_start(out=wk_raw[:], in_=wk_words[0].bitcast(I32))
 
-        def load_w8():
-            nc.sync.dma_start(out=w8_raw[:], in_=w8_words[0].rearrange("p n t -> p (n t)").bitcast(I32))
+        def load_w8(eng="sync"):
+            queue[eng].dma_start(out=w8_raw[:], in_=w8_words[0].rearrange("p n t -> p (n t)").bitcast(I32))
 
         def load_scales(name, eng="sync", quadrants=range(4)):
             dram, col0 = w_scales[name]
@@ -80,29 +82,40 @@ def tile_mix_kvw_relu_kernel(
             for e in range(col0 // EIGHTH, (col0 + width) // EIGHTH):
                 raw_piece[name, e] = (piece, col0)
 
-        def deal_wk():
-            nc.vector.tensor_copy(
-                out=wk_codes[:].bitcast(U16).rearrange("p (t g i) -> p g t i", t=PACK, i=8),
-                in_=wk_raw[:].bitcast(U16).rearrange("p (g i t) -> p g t i", t=PACK, i=8),
+        def move(eng, out, in_):
+            if eng == "vector":
+                nc.vector.tensor_copy(out=out, in_=in_)
+            else:
+                nc.scalar.copy(out=out, in_=in_)
+
+        def deal_wk(eng="vector", h0=0, h1=2):
+            home = wk_whole if h1 - h0 == 2 else wk_codes[h0]
+            for t in range(2 * h0, 2 * h1):
+                wk_view[t] = home[:, 2 * P * (t - 2 * h0) : 2 * P * (t - 2 * h0 + 1)]
+            move(
+                eng,
+                home[:].bitcast(U16).rearrange("p (t g i) -> p g t i", t=2 * (h1 - h0), i=8),
+                wk_raw[:].bitcast(U16).rearrange("p (g i t) -> p g t i", t=PACK, i=8)[:, :, 2 * h0 : 2 * h1, :],
             )
 
         def deal_wk_plane(h):
             nc.vector.tensor_copy(
-                out=wk_plane[h][:].rearrange("p (t g i) -> p g t i", t=2, i=16),
-                in_=scales_raw[:, 0:D].rearrange("p (g i t) -> p g t i", t=PACK, i=16)[:, :, 2 * h : 2 * h + 2, :],
+                out=wk_plane[h][:].rearrange("p (t m) -> p t m", t=2),
+                in_=scales_raw[:, 0:D].rearrange("p (m t) -> p t m", t=PACK)[:, 2 * h : 2 * h + 2, :],
             )
 
-        def deal_w8():
-            nc.vector.tensor_copy(
-                out=w8_codes[:].rearrange("p (t g i) -> p g t i", t=PACK, i=4),
-                in_=w8_raw[:].rearrange("p (g i t) -> p g t i", t=PACK, i=4),
+        def deal_w8(eng="vector"):
+            move(
+                eng,
+                w8_codes[:].bitcast(U32).rearrange("p (u e g i) -> p g u i e", u=2, e=2, i=4),
+                w8_raw[:].bitcast(U32).rearrange("p (g i u e) -> p g u i e", u=2, e=2, i=4),
             )
 
         def deal_plane(name, t0=0, t1=PACK):
             col0 = w_scales[name][1]
             nc.vector.tensor_copy(
-                out=w_plane[name][:].rearrange("p (t g i) -> p g t i", t=PACK, i=16)[:, :, t0:t1, :],
-                in_=scales_raw[:, col0 : col0 + D].rearrange("p (g i t) -> p g t i", t=PACK, i=16)[:, :, t0:t1, :],
+                out=w_plane[name][:].rearrange("p (t m) -> p t m", t=PACK)[:, t0:t1, :],
+                in_=scales_raw[:, col0 : col0 + D].rearrange("p (m t) -> p t m", t=PACK)[:, t0:t1, :],
             )
 
         def round_cols(eng, name, col0, width):
@@ -121,21 +134,21 @@ def tile_mix_kvw_relu_kernel(
                 in_=bf[name][:, PACK * col0 : PACK * (col0 + width)],
             )
 
-        def project(name, q, t0=0, t1=PACK):
-            cols = slice(q * QUARTER, (q + 1) * QUARTER)
-            result = {"c": "kc", "x": "qr"}[name]
-            home = q if name == "c" else 4 + q
-            if t0 == 0:
-                acc[result, q] = ps.tile([P, PACK, QUARTER], F32, name="bank%d" % home)
+        def project_cols(name, col0, width, t0, t1, b, first=True):
+            cols = slice(col0, col0 + width)
+            if first:
+                acc[name, col0, t0] = ps.tile([P, PACK, width], F32, name="bank%d" % b)
+            else:
+                acc[name, col0, t0] = acc[name, col0, 0]
             for t in range(t0, t1):
                 if name == "c":
-                    lhsT = wk_codes[:, 2 * P * t : 2 * P * (t + 1)].bitcast(FP4X4)
+                    lhsT = wk_view[t].bitcast(FP4X4)
                     lhsT_scale = wk_plane[t // 2][:, P * (t % 2) : P * (t % 2 + 1)]
                 else:
                     lhsT = w8_codes[:, P * t : P * (t + 1)].bitcast(FP8X4)
                     lhsT_scale = w_plane["w8"][:, P * t : P * (t + 1)]
                 nc.tensor.matmul_mx(
-                    out=acc[result, q][:, t, :],
+                    out=acc[name, col0, t0][:, t, :],
                     lhsT=lhsT,
                     lhsT_scale=lhsT_scale,
                     rhs=codes[name][:, cols].bitcast(FP8X4),
@@ -144,27 +157,18 @@ def tile_mix_kvw_relu_kernel(
                     stop=True,
                 )
 
-        def project_part(col0, width, b):
-            cols = slice(col0, col0 + width)
-            acc["qr", col0, width] = ps.tile([P, PACK, width], F32, name="bank%d" % b)
-            for t in range(PACK):
-                nc.tensor.matmul_mx(
-                    out=acc["qr", col0, width][:, t, :],
-                    lhsT=w8_codes[:, P * t : P * (t + 1)].bitcast(FP8X4),
-                    lhsT_scale=w_plane["w8"][:, P * t : P * (t + 1)],
-                    rhs=codes["x"][:, cols].bitcast(FP8X4),
-                    rhs_scale=plane["x"][:, cols],
-                    start=True,
-                    stop=True,
-                )
+        def project(name, q, t0=0, t1=PACK):
+            project_cols(name, q * QUARTER, QUARTER, t0, t1, q if name == "c" else 4 + q, t0 == 0)
+            acc[{"c": "kc", "x": "qr"}[name], q] = acc[name, q * QUARTER, 0]
 
-        def drain_part(eng, col0, width):
-            out = bf["qr"][:, PACK * col0 : PACK * (col0 + width)].rearrange("p (n t) -> p n t", t=PACK)
-            in_ = acc["qr", col0, width][:].rearrange("p t n -> p n t")
-            if eng == "vector":
-                nc.vector.tensor_copy(out=out, in_=in_)
-            else:
-                nc.scalar.copy(out=out, in_=in_)
+        def keys_cols(eng, col0, width, t0, t1):
+            piece, base = raw_piece["kc", col0 // EIGHTH]
+            move(eng, piece[:, t0:t1, col0 - base : col0 - base + width], acc.get(("c", col0, t0), acc["c", col0, 0])[:, t0:t1, :])
+
+        def round_bank(eng, name, col0, width):
+            result = {"c": "kc", "x": "qr"}[name]
+            out = bf[result][:, PACK * col0 : PACK * (col0 + width)].rearrange("p (n t) -> p n t", t=PACK)
+            move(eng, out, acc[name, col0, 0][:].rearrange("p t n -> p n t"))
 
         def score(q, col0=0, width=J, b=None):
             rows = slice(q * QUARTER, (q + 1) * QUARTER)
@@ -208,17 +212,17 @@ def tile_mix_kvw_relu_kernel(
                 out=out_0[q * QUARTER : (q + 1) * QUARTER, col0 : col0 + width], in_=scores[q][:, col0 : col0 + width]
             )
 
-        def store_keys(col0, width):
+        def store_keys(col0, width, eng="sync"):
             view = out_1.rearrange("(p t) n -> p t n", t=PACK)
             piece, base = raw_piece["kc", col0 // EIGHTH]
-            nc.sync.dma_start(out=view[:, :, col0 : col0 + width], in_=piece[:, :, col0 - base : col0 - base + width])
+            queue[eng].dma_start(out=view[:, :, col0 : col0 + width], in_=piece[:, :, col0 - base : col0 - base + width])
 
-        def store_codes(col0=0, width=J):
+        def store_codes(col0=0, width=J, eng="sync"):
             words = out_2[0].rearrange("p n t -> p (n t)").bitcast(I32)
-            nc.sync.dma_start(out=words[:, col0 : col0 + width], in_=codes["kc"][:, col0 : col0 + width].bitcast(I32))
+            queue[eng].dma_start(out=words[:, col0 : col0 + width], in_=codes["kc"][:, col0 : col0 + width].bitcast(I32))
 
-        def store_plane(eng="sync"):
-            for q in range(4):
+        def store_plane(eng="sync", quadrants=range(4)):
+            for q in quadrants:
                 queue[eng].dma_start(
                     out=out_3[0].bitcast(I32)[q:16:4, :], in_=plane["kc"][q:P:32, :].bitcast(I32)
                 )

@@ -32,7 +32,7 @@ def tile_mix_kvw_relu_kernel(
         sb = ctx.enter_context(tc.tile_pool(name="sb", bufs=1))
         ps = ctx.enter_context(tc.psum_pool(name="ps", bufs=1))
         ctx.enter_context(tc.manual_schedule())
-        queue = {"sync": nc.sync, "scalar": nc.scalar, "gpsimd": nc.gpsimd}
+        queue = {"sync": nc.sync, "scalar": nc.scalar}
 
         def tile(name, shape, dtype):
             return sb.tile(shape, dtype, name=name, align_bytes=64)
@@ -40,9 +40,7 @@ def tile_mix_kvw_relu_kernel(
         wk_raw = tile("wk_raw", [P, D // 2], I32)
         w8_raw = tile("w8_raw", [P, D], I32)
         scales_raw = tile("scales_raw", [P, 2 * D], U8)
-        wk_codes = [tile("wk_codes%d" % h, [P, D], U8) for h in range(2)]
-        wk_whole = tile("wk_whole", [P, 2 * D], U8)
-        wk_view = {}
+        wk_codes = tile("wk_codes", [P, 2 * D], U8)
         wk_plane = [tile("wk_plane%d" % h, [P, HALF], U8) for h in range(2)]
         w8_codes = tile("w8_codes", [P, D], I32)
         w_plane = {"w8": tile("w8_plane", [P, D], U8)}
@@ -60,11 +58,11 @@ def tile_mix_kvw_relu_kernel(
         def zero_scales():
             nc.vector.memset(scales_raw[:].bitcast(I32), 0)
 
-        def load_wk(eng="sync"):
-            queue[eng].dma_start(out=wk_raw[:], in_=wk_words[0].bitcast(I32))
+        def load_wk():
+            nc.sync.dma_start(out=wk_raw[:], in_=wk_words[0].bitcast(I32))
 
-        def load_w8(eng="sync"):
-            queue[eng].dma_start(out=w8_raw[:], in_=w8_words[0].rearrange("p n t -> p (n t)").bitcast(I32))
+        def load_w8():
+            nc.sync.dma_start(out=w8_raw[:], in_=w8_words[0].rearrange("p n t -> p (n t)").bitcast(I32))
 
         def load_scales(name, eng="sync", quadrants=range(4)):
             dram, col0 = w_scales[name]
@@ -82,20 +80,10 @@ def tile_mix_kvw_relu_kernel(
             for e in range(col0 // EIGHTH, (col0 + width) // EIGHTH):
                 raw_piece[name, e] = (piece, col0)
 
-        def move(eng, out, in_):
-            if eng == "vector":
-                nc.vector.tensor_copy(out=out, in_=in_)
-            else:
-                nc.scalar.copy(out=out, in_=in_)
-
-        def deal_wk(eng="vector", h0=0, h1=2):
-            home = wk_whole if h1 - h0 == 2 else wk_codes[h0]
-            for t in range(2 * h0, 2 * h1):
-                wk_view[t] = home[:, 2 * P * (t - 2 * h0) : 2 * P * (t - 2 * h0 + 1)]
-            move(
-                eng,
-                home[:].bitcast(U16).rearrange("p (t g i) -> p g t i", t=2 * (h1 - h0), i=8),
-                wk_raw[:].bitcast(U16).rearrange("p (g i t) -> p g t i", t=PACK, i=8)[:, :, 2 * h0 : 2 * h1, :],
+        def deal_wk():
+            nc.vector.tensor_copy(
+                out=wk_codes[:].bitcast(U16).rearrange("p (t g i) -> p g t i", t=PACK, i=8),
+                in_=wk_raw[:].bitcast(U16).rearrange("p (g i t) -> p g t i", t=PACK, i=8),
             )
 
         def deal_wk_plane(h):
@@ -104,11 +92,10 @@ def tile_mix_kvw_relu_kernel(
                 in_=scales_raw[:, 0:D].rearrange("p (m t) -> p t m", t=PACK)[:, 2 * h : 2 * h + 2, :],
             )
 
-        def deal_w8(eng="vector"):
-            move(
-                eng,
-                w8_codes[:].bitcast(U32).rearrange("p (u e g i) -> p g u i e", u=2, e=2, i=4),
-                w8_raw[:].bitcast(U32).rearrange("p (g i u e) -> p g u i e", u=2, e=2, i=4),
+        def deal_w8():
+            nc.vector.tensor_copy(
+                out=w8_codes[:].rearrange("p (u e g i) -> p g u i e", u=2, e=2, i=4),
+                in_=w8_raw[:].rearrange("p (g i u e) -> p g u i e", u=2, e=2, i=4),
             )
 
         def deal_plane(name, t0=0, t1=PACK):
@@ -134,21 +121,21 @@ def tile_mix_kvw_relu_kernel(
                 in_=bf[name][:, PACK * col0 : PACK * (col0 + width)],
             )
 
-        def project_cols(name, col0, width, t0, t1, b, first=True):
-            cols = slice(col0, col0 + width)
-            if first:
-                acc[name, col0, t0] = ps.tile([P, PACK, width], F32, name="bank%d" % b)
-            else:
-                acc[name, col0, t0] = acc[name, col0, 0]
+        def project(name, q, t0=0, t1=PACK):
+            cols = slice(q * QUARTER, (q + 1) * QUARTER)
+            result = {"c": "kc", "x": "qr"}[name]
+            home = q if name == "c" else 4 + q
+            if t0 == 0:
+                acc[result, q] = ps.tile([P, PACK, QUARTER], F32, name="bank%d" % home)
             for t in range(t0, t1):
                 if name == "c":
-                    lhsT = wk_view[t].bitcast(FP4X4)
+                    lhsT = wk_codes[:, 2 * P * t : 2 * P * (t + 1)].bitcast(FP4X4)
                     lhsT_scale = wk_plane[t // 2][:, P * (t % 2) : P * (t % 2 + 1)]
                 else:
                     lhsT = w8_codes[:, P * t : P * (t + 1)].bitcast(FP8X4)
                     lhsT_scale = w_plane["w8"][:, P * t : P * (t + 1)]
                 nc.tensor.matmul_mx(
-                    out=acc[name, col0, t0][:, t, :],
+                    out=acc[result, q][:, t, :],
                     lhsT=lhsT,
                     lhsT_scale=lhsT_scale,
                     rhs=codes[name][:, cols].bitcast(FP8X4),
@@ -157,18 +144,27 @@ def tile_mix_kvw_relu_kernel(
                     stop=True,
                 )
 
-        def project(name, q, t0=0, t1=PACK):
-            project_cols(name, q * QUARTER, QUARTER, t0, t1, q if name == "c" else 4 + q, t0 == 0)
-            acc[{"c": "kc", "x": "qr"}[name], q] = acc[name, q * QUARTER, 0]
+        def project_part(col0, width, b):
+            cols = slice(col0, col0 + width)
+            acc["qr", col0, width] = ps.tile([P, PACK, width], F32, name="bank%d" % b)
+            for t in range(PACK):
+                nc.tensor.matmul_mx(
+                    out=acc["qr", col0, width][:, t, :],
+                    lhsT=w8_codes[:, P * t : P * (t + 1)].bitcast(FP8X4),
+                    lhsT_scale=w_plane["w8"][:, P * t : P * (t + 1)],
+                    rhs=codes["x"][:, cols].bitcast(FP8X4),
+                    rhs_scale=plane["x"][:, cols],
+                    start=True,
+                    stop=True,
+                )
 
-        def keys_cols(eng, col0, width, t0, t1):
-            piece, base = raw_piece["kc", col0 // EIGHTH]
-            move(eng, piece[:, t0:t1, col0 - base : col0 - base + width], acc.get(("c", col0, t0), acc["c", col0, 0])[:, t0:t1, :])
-
-        def round_bank(eng, name, col0, width):
-            result = {"c": "kc", "x": "qr"}[name]
-            out = bf[result][:, PACK * col0 : PACK * (col0 + width)].rearrange("p (n t) -> p n t", t=PACK)
-            move(eng, out, acc[name, col0, 0][:].rearrange("p t n -> p n t"))
+        def drain_part(eng, col0, width):
+            out = bf["qr"][:, PACK * col0 : PACK * (col0 + width)].rearrange("p (n t) -> p n t", t=PACK)
+            in_ = acc["qr", col0, width][:].rearrange("p t n -> p n t")
+            if eng == "vector":
+                nc.vector.tensor_copy(out=out, in_=in_)
+            else:
+                nc.scalar.copy(out=out, in_=in_)
 
         def score(q, col0=0, width=J, b=None):
             rows = slice(q * QUARTER, (q + 1) * QUARTER)
@@ -212,17 +208,17 @@ def tile_mix_kvw_relu_kernel(
                 out=out_0[q * QUARTER : (q + 1) * QUARTER, col0 : col0 + width], in_=scores[q][:, col0 : col0 + width]
             )
 
-        def store_keys(col0, width, eng="sync"):
+        def store_keys(col0, width):
             view = out_1.rearrange("(p t) n -> p t n", t=PACK)
             piece, base = raw_piece["kc", col0 // EIGHTH]
-            queue[eng].dma_start(out=view[:, :, col0 : col0 + width], in_=piece[:, :, col0 - base : col0 - base + width])
+            nc.sync.dma_start(out=view[:, :, col0 : col0 + width], in_=piece[:, :, col0 - base : col0 - base + width])
 
-        def store_codes(col0=0, width=J, eng="sync"):
+        def store_codes(col0=0, width=J):
             words = out_2[0].rearrange("p n t -> p (n t)").bitcast(I32)
-            queue[eng].dma_start(out=words[:, col0 : col0 + width], in_=codes["kc"][:, col0 : col0 + width].bitcast(I32))
+            nc.sync.dma_start(out=words[:, col0 : col0 + width], in_=codes["kc"][:, col0 : col0 + width].bitcast(I32))
 
-        def store_plane(eng="sync", quadrants=range(4)):
-            for q in quadrants:
+        def store_plane(eng="sync"):
+            for q in range(4):
                 queue[eng].dma_start(
                     out=out_3[0].bitcast(I32)[q:16:4, :], in_=plane["kc"][q:P:32, :].bitcast(I32)
                 )

@@ -22,6 +22,7 @@ EIGHTH = 64
 QUARTER = 128
 HALF = 256
 SCORE_SCALE = 0.03125
+ROW = 2048
 
 
 def tile_mix_kvw_relu_kernel(
@@ -34,11 +35,11 @@ def tile_mix_kvw_relu_kernel(
         ctx.enter_context(tc.manual_schedule())
         queue = {"sync": nc.sync, "scalar": nc.scalar}
 
-        def tile(name, shape, dtype):
-            return sb.tile(shape, dtype, name=name, align_bytes=64)
+        def tile(name, shape, dtype, align=256):
+            return sb.tile(shape, dtype, name=name, align_bytes=align)
 
-        wk_raw = tile("wk_raw", [P, D // 2], I32)
-        w8_raw = tile("w8_raw", [P, D], I32)
+        wk_raw = tile("wk_raw", [P, D // 2], I32, ROW)
+        w8_raw = tile("w8_raw", [P, D], I32, ROW)
         scales_raw = tile("scales_raw", [P, 2 * D], U8)
         wk_codes = tile("wk_codes", [P, 2 * D], U8)
         wk_plane = [tile("wk_plane%d" % h, [P, HALF], U8) for h in range(2)]
@@ -46,13 +47,13 @@ def tile_mix_kvw_relu_kernel(
         w_plane = {"w8": tile("w8_plane", [P, D], U8)}
         w_scales = {"wk": (wk_scales, 0), "w8": (w8_scales, D)}
         acts = {"c": c, "x": x}
-        kc_f32 = [tile("kc_f32_%d" % h, [P, PACK, HALF], F32) for h in range(2)]
+        kc_f32 = [tile("kc_f32_%d" % h, [P, PACK, HALF], F32, ROW) for h in range(2)]
         raw = {("kc", q): kc_f32[q // 2][:, :, (q % 2) * QUARTER : (q % 2 + 1) * QUARTER] for q in range(4)}
         raw_piece = {("kc", e): (kc_f32[e // 4], (e // 4) * HALF) for e in range(8)}
-        bf = {name: tile(name + "_bf", [P, PACK * M], BF16) for name in ("c", "x", "kc", "qr")}
-        codes = {name: tile(name + "_codes", [P, M], U32) for name in ("c", "x", "kc", "qr")}
+        bf = {name: tile(name + "_bf", [P, PACK * M], BF16, ROW) for name in ("c", "x", "kc", "qr")}
+        codes = {name: tile(name + "_codes", [P, M], U32, ROW) for name in ("c", "x", "kc", "qr")}
         plane = {name: tile(name + "_plane", [P, M], U8) for name in ("c", "x", "kc", "qr")}
-        scores = [tile("scores%d" % q, [P, J], F32) for q in range(4)]
+        scores = [tile("scores%d" % q, [P, J], F32, ROW) for q in range(4)]
         acc = {}
 
         def zero_scales():
@@ -74,7 +75,7 @@ def tile_mix_kvw_relu_kernel(
                 )
 
         def load(name, col0, width, eng="sync"):
-            piece = tile("%s_raw%d" % (name, col0), [P, PACK, width], F32)
+            piece = tile("%s_raw%d" % (name, col0), [P, PACK, width], F32, ROW)
             view = acts[name].rearrange("(p t) n -> p t n", t=PACK)
             queue[eng].dma_start(out=piece[:], in_=view[:, :, col0 : col0 + width])
             for e in range(col0 // EIGHTH, (col0 + width) // EIGHTH):

@@ -187,6 +187,12 @@ def tile_mix_kvw_relu_kernel(
             else:
                 nc.scalar.copy(out=raw["kc", q], in_=acc["kc", q][:])
 
+        def keys_rows(eng, q, t0, t1):
+            if eng == "vector":
+                nc.vector.tensor_copy(out=raw["kc", q][:, t0:t1, :], in_=acc["kc", q][:, t0:t1, :])
+            else:
+                nc.scalar.copy(out=raw["kc", q][:, t0:t1, :], in_=acc["kc", q][:, t0:t1, :])
+
         def drain_round(eng, name, q):
             out = bf[name][:, PACK * QUARTER * q : PACK * QUARTER * (q + 1)].rearrange("p (n t) -> p n t", t=PACK)
             in_ = acc[name, q][:].rearrange("p t n -> p n t")
@@ -239,7 +245,6 @@ def tile_mix_kvw_relu_kernel(
                 drain_scores(engines[h], q, h * HALF, HALF)
             store_scores(q)
 
-
         zero_scales()
         load_wk()
         load("c", 0, Q)
@@ -282,20 +287,20 @@ def tile_mix_kvw_relu_kernel(
         store_keys(HALF, Q)
         drain_round(S, "kc", 3)
         drain_round(S, "qr", 0)
-        drain_keys(S, 3)
-        round_cols(V, "kc", Q, Q)
         round_cols(V, "x", Q, Q)
-        quantize("kc", 0, HALF)
+        round_cols(V, "kc", Q, Q)
         quantize("x", Q, Q)
         project("x", 1)
         drain_round(S, "qr", 1)
+        drain_keys(S, 3)
         round_cols(V, "x", 2 * Q, Q)
+        quantize("kc", 0, HALF)
+        quantize("x", 2 * Q, Q)
+        project("x", 2)
         quantize("kc", HALF, HALF)
         store_codes()
         store_plane()
         store_keys(3 * Q, Q)
-        quantize("x", 2 * Q, Q)
-        project("x", 2)
         drain_round(S, "qr", 2)
         round_cols(V, "x", 3 * Q, Q)
         quantize("qr", 0, Q)

from contextlib import ExitStack

import concourse.mybir as mybir

K, D, M, J = 512, 512, 512, 512
FLOPS = 2 * (K * D * M + K * D * J + D * M * J)

F32 = mybir.dt.float32
BF16 = mybir.dt.bfloat16
I32 = mybir.dt.int32
U32 = mybir.dt.uint32
U16 = mybir.dt.uint16
U8 = mybir.dt.uint8
FP8X4 = mybir.dt.float8_e4m3fn_x4
FP4X4 = mybir.dt.float4_e2m1fn_x4
ACT = mybir.ActivationFunctionType
ALU = mybir.AluOpType

P = 128
PACK = 4
EIGHTH = 64
QUARTER = 128
HALF = 256
SCORE_SCALE = 0.03125
ROW = 2048


def tile_mix_kvw_relu_kernel(
    tc, x, w8_words, w8_scales, c, wk_words, wk_scales, out_0, out_1, out_2, out_3
):
    nc = tc.nc
    with ExitStack() as ctx:
        sb = ctx.enter_context(tc.tile_pool(name="sb", bufs=1))
        ps = ctx.enter_context(tc.psum_pool(name="ps", bufs=1))
        ctx.enter_context(tc.manual_schedule())
        queue = {"sync": nc.sync, "scalar": nc.scalar}

        def tile(name, shape, dtype, align=256):
            return sb.tile(shape, dtype, name=name, align_bytes=align)

        wk_raw = tile("wk_raw", [P, D // 2], I32, ROW)
        w8_raw = tile("w8_raw", [P, D], I32, ROW)
        scales_raw = tile("scales_raw", [P, 2 * D], U8)
        wk_codes = tile("wk_codes", [P, 2 * D], U8)
        wk_plane = [tile("wk_plane%d" % h, [P, HALF], U8) for h in range(2)]
        w8_codes = tile("w8_codes", [P, D], I32)
        w_plane = {"w8": tile("w8_plane", [P, D], U8)}
        w_scales = {"wk": (wk_scales, 0), "w8": (w8_scales, D)}
        acts = {"c": c, "x": x}
        kc_f32 = [tile("kc_f32_%d" % h, [P, PACK, HALF], F32, ROW) for h in range(2)]
        raw = {("kc", q): kc_f32[q // 2][:, :, (q % 2) * QUARTER : (q % 2 + 1) * QUARTER] for q in range(4)}
        raw_piece = {("kc", e): (kc_f32[e // 4], (e // 4) * HALF) for e in range(8)}
        bf = {name: tile(name + "_bf", [P, PACK * M], BF16, ROW) for name in ("c", "x", "kc", "qr")}
        codes = {name: tile(name + "_codes", [P, M], U32, ROW) for name in ("c", "x", "kc", "qr")}
        plane = {name: tile(name + "_plane", [P, M], U8) for name in ("c", "x", "kc", "qr")}
        scores = [tile("scores%d" % q, [P, J], F32, ROW) for q in range(4)]
        acc = {}

        def zero_scales():
            nc.vector.memset(scales_raw[:].bitcast(I32), 0)

        def load_wk():
            nc.sync.dma_start(out=wk_raw[:], in_=wk_words[0].bitcast(I32))

        def load_w8():
            nc.sync.dma_start(out=w8_raw[:], in_=w8_words[0].rearrange("p n t -> p (n t)").bitcast(I32))

        def load_scales(name, eng="sync", quadrants=range(4)):
            dram, col0 = w_scales[name]
            rows = dram[0].bitcast(I32)
            for q in quadrants:
                queue[eng].dma_start(
                    out=scales_raw[q:P:32, col0 : col0 + D].bitcast(I32),
                    in_=rows[q:16:4, :],
                )

        def load(name, col0, width, eng="sync"):
            piece = tile("%s_raw%d" % (name, col0), [P, PACK, width], F32, ROW)
            view = acts[name].rearrange("(p t) n -> p t n", t=PACK)
            queue[eng].dma_start(out=piece[:], in_=view[:, :, col0 : col0 + width])
            for e in range(col0 // EIGHTH, (col0 + width) // EIGHTH):
                raw_piece[name, e] = (piece, col0)

        def deal_wk():
            nc.vector.tensor_copy(
                out=wk_codes[:].bitcast(U16).rearrange("p (t g i) -> p g t i", t=PACK, i=8),
                in_=wk_raw[:].bitcast(U16).rearrange("p (g i t) -> p g t i", t=PACK, i=8),
            )

        def deal_wk_plane(h):
            nc.vector.tensor_copy(
                out=wk_plane[h][:].rearrange("p (t m) -> p t m", t=2),
                in_=scales_raw[:, 0:D].rearrange("p (m t) -> p t m", t=PACK)[:, 2 * h : 2 * h + 2, :],
            )

        def deal_w8():
            nc.vector.tensor_copy(
                out=w8_codes[:].rearrange("p (u e g i) -> p g u i e", u=2, e=2, i=4),
                in_=w8_raw[:].rearrange("p (g i u e) -> p g u i e", u=2, e=2, i=4),
            )

        def deal_plane(name, t0=0, t1=PACK):
            col0 = w_scales[name][1]
            nc.vector.tensor_copy(
                out=w_plane[name][:].rearrange("p (t m) -> p t m", t=PACK)[:, t0:t1, :],
                in_=scales_raw[:, col0 : col0 + D].rearrange("p (m t) -> p t m", t=PACK)[:, t0:t1, :],
            )

        def round_cols(eng, name, col0, width):
            piece, base = raw_piece[name, col0 // EIGHTH]
            out = bf[name][:, PACK * col0 : PACK * (col0 + width)].rearrange("p (g i t) -> p g t i", t=PACK, i=4)
            in_ = piece[:, :, col0 - base : col0 - base + width].rearrange("p t (g i) -> p g t i", i=4)
            if eng == "vector":
                nc.vector.tensor_copy(out=out, in_=in_)
            else:
                nc.scalar.activation(out=out, in_=in_, func=ACT.Copy)

        def quantize(name, col0, width):
            nc.vector.quantize_mx(
                out=codes[name][:, col0 : col0 + width].bitcast(FP8X4),
                scales=plane[name][:, col0 : col0 + width],
                in_=bf[name][:, PACK * col0 : PACK * (col0 + width)],
            )

        def project(name, q, t0=0, t1=PACK):
            cols = slice(q * QUARTER, (q + 1) * QUARTER)
            result = {"c": "kc", "x": "qr"}[name]
            home = q if name == "c" else 4 + q
            if t0 == 0:
                acc[result, q] = ps.tile([P, PACK, QUARTER], F32, name="bank%d" % home)
            for t in range(t0, t1):
                if name == "c":
                    lhsT = wk_codes[:, 2 * P * t : 2 * P * (t + 1)].bitcast(FP4X4)
                    lhsT_scale = wk_plane[t // 2][:, P * (t % 2) : P * (t % 2 + 1)]
                else:
                    lhsT = w8_codes[:, P * t : P * (t + 1)].bitcast(FP8X4)
                    lhsT_scale = w_plane["w8"][:, P * t : P * (t + 1)]
                nc.tensor.matmul_mx(
                    out=acc[result, q][:, t, :],
                    lhsT=lhsT,
                    lhsT_scale=lhsT_scale,
                    rhs=codes[name][:, cols].bitcast(FP8X4),
                    rhs_scale=plane[name][:, cols],
                    start=True,
                    stop=True,
                )

        def project_part(col0, width, b):
            cols = slice(col0, col0 + width)
            acc["qr", col0, width] = ps.tile([P, PACK, width], F32, name="bank%d" % b)
            for t in range(PACK):
                nc.tensor.matmul_mx(
                    out=acc["qr", col0, width][:, t, :],
                    lhsT=w8_codes[:, P * t : P * (t + 1)].bitcast(FP8X4),
                    lhsT_scale=w_plane["w8"][:, P * t : P * (t + 1)],
                    rhs=codes["x"][:, cols].bitcast(FP8X4),
                    rhs_scale=plane["x"][:, cols],
                    start=True,
                    stop=True,
                )

        def drain_part(eng, col0, width):
            out = bf["qr"][:, PACK * col0 : PACK * (col0 + width)].rearrange("p (n t) -> p n t", t=PACK)
            in_ = acc["qr", col0, width][:].rearrange("p t n -> p n t")
            if eng == "vector":
                nc.vector.tensor_copy(out=out, in_=in_)
            else:
                nc.scalar.copy(out=out, in_=in_)

        def score(q, col0=0, width=J, b=None):
            rows = slice(q * QUARTER, (q + 1) * QUARTER)
            cols = slice(col0, col0 + width)
            acc["sc", q, col0] = ps.tile([P, width], F32, name="bank%d" % (q if b is None else b))
            nc.tensor.matmul_mx(
                out=acc["sc", q, col0][:],
                lhsT=codes["qr"][:, rows].bitcast(FP8X4),
                lhsT_scale=plane["qr"][:, rows],
                rhs=codes["kc"][:, cols].bitcast(FP8X4),
                rhs_scale=plane["kc"][:, cols],
                start=True,
                stop=True,
            )

        def drain_keys(eng, q):
            if eng == "vector":
                nc.vector.tensor_copy(out=raw["kc", q], in_=acc["kc", q][:])
            else:
                nc.scalar.copy(out=raw["kc", q], in_=acc["kc", q][:])

        def keys_rows(eng, q, t0, t1):
            if eng == "vector":
                nc.vector.tensor_copy(out=raw["kc", q][:, t0:t1, :], in_=acc["kc", q][:, t0:t1, :])
            else:
                nc.scalar.copy(out=raw["kc", q][:, t0:t1, :], in_=acc["kc", q][:, t0:t1, :])

        def drain_round(eng, name, q):
            out = bf[name][:, PACK * QUARTER * q : PACK * QUARTER * (q + 1)].rearrange("p (n t) -> p n t", t=PACK)
            in_ = acc[name, q][:].rearrange("p t n -> p n t")
            if eng == "vector":
                nc.vector.tensor_copy(out=out, in_=in_)
            else:
                nc.scalar.copy(out=out, in_=in_)

        def drain_scores(eng, q, col0=0, width=J):
            out = scores[q][:, col0 : col0 + width]
            if eng == "vector":
                nc.vector.tensor_scalar(
                    out=out, in0=acc["sc", q, col0][:], scalar1=0.0, scalar2=SCORE_SCALE, op0=ALU.max, op1=ALU.mult
                )
            else:
                nc.scalar.activation(out=out, in_=acc["sc", q, col0][:], func=ACT.Relu, scale=SCORE_SCALE)

        def store_scores(q, col0=0, width=J, eng="sync"):
            queue[eng].dma_start(
                out=out_0[q * QUARTER : (q + 1) * QUARTER, col0 : col0 + width], in_=scores[q][:, col0 : col0 + width]
            )

        def store_keys(col0, width):
            view = out_1.rearrange("(p t) n -> p t n", t=PACK)
            piece, base = raw_piece["kc", col0 // EIGHTH]
            nc.sync.dma_start(out=view[:, :, col0 : col0 + width], in_=piece[:, :, col0 - base : col0 - base + width])

        def store_codes(col0=0, width=J):
            words = out_2[0].rearrange("p n t -> p (n t)").bitcast(I32)
            nc.sync.dma_start(out=words[:, col0 : col0 + width], in_=codes["kc"][:, col0 : col0 + width].bitcast(I32))

        def store_plane(eng="sync"):
            for q in range(4):
                queue[eng].dma_start(
                    out=out_3[0].bitcast(I32)[q:16:4, :], in_=plane["kc"][q:P:32, :].bitcast(I32)
                )

        V, S, Q = "vector", "scalar", QUARTER

        def round_shared(name, q, share=Q // 2):
            round_cols(V, name, q * Q, share)
            round_cols(S, name, q * Q + share, Q - share)

        def score_tile(q):
            score(q, 0, HALF, 4 + q)
            score(q, HALF, HALF, q)

        def finish(q, engines):
            for h in range(2):
                drain_scores(engines[h], q, h * HALF, HALF)
            store_scores(q)

        zero_scales()
        load_wk()
        load("c", 0, Q)
        load_scales("wk")
        for q in range(1, 4):
            load("c", q * Q, Q)
        load("x", 0, Q)
        load_scales("w8")
        load_w8()
        for q in range(1, 4):
            load("x", q * Q, Q)

        deal_wk()
        round_shared("c", 0, 88)
        deal_wk_plane(0)
        quantize("c", 0, Q)
        project("c", 0, 0, 2)
        deal_wk_plane(1)
        project("c", 0, 2, 4)
        round_shared("c", 1, 88)
        quantize("c", Q, Q)
        project("c", 1)
        round_cols(V, "c", 2 * Q, Q)
        quantize("c", 2 * Q, Q)
        project("c", 2)
        round_cols(V, "c", 3 * Q, Q)
        round_cols(V, "x", 0, Q)
        quantize("c", 3 * Q, Q)
        project("c", 3)
        deal_plane("w8")
        quantize("x", 0, Q)
        deal_w8()
        project("x", 0)
        drain_round(S, "kc", 0)
        drain_keys(S, 0)
        drain_keys(S, 1)
        store_keys(0, HALF)
        drain_round(S, "kc", 2)
        drain_keys(S, 2)
        store_keys(HALF, Q)
        drain_round(S, "kc", 3)
        drain_round(S, "qr", 0)
        round_cols(V, "x", Q, Q)
        round_cols(V, "kc", Q, Q)
        quantize("x", Q, Q)
        project("x", 1)
        drain_round(S, "qr", 1)
        drain_keys(S, 3)
        round_cols(V, "x", 2 * Q, Q)
        quantize("kc", 0, HALF)
        quantize("x", 2 * Q, Q)
        project("x", 2)
        quantize("kc", HALF, HALF)
        store_codes()
        store_plane()
        store_keys(3 * Q, Q)
        drain_round(S, "qr", 2)
        round_cols(V, "x", 3 * Q, Q)
        quantize("qr", 0, Q)
        score_tile(0)
        quantize("x", 3 * Q, Q)
        project("x", 3)
        drain_round(S, "qr", 3)
        quantize("qr", Q, Q)
        score_tile(1)
        finish(0, (V, V))
        quantize("qr", 2 * Q, Q)
        score_tile(2)
        drain_scores(V, 1, 0, HALF)
        quantize("qr", 3 * Q, Q)
        score_tile(3)
        drain_scores(S, 1, HALF, HALF)
        store_scores(1)
        finish(2, (S, V))
        finish(3, (S, V))
